import numpy as np
import ml_dtypes


def mxq(x, axis, fmt="e4m3"):
    dtype, down = {"e4m3": (ml_dtypes.float8_e4m3fn, 7), "e5m2": (ml_dtypes.float8_e5m2, 14)}[fmt]
    v = np.moveaxis(np.asarray(x, np.float32).astype(ml_dtypes.bfloat16).astype(np.float64), axis, -1)
    blocks = v.reshape(v.shape[:-1] + (-1, 32))
    amax = np.abs(blocks).max(-1, keepdims=True)
    byte = np.maximum(np.where(amax > 0, np.frexp(amax)[1] - 1 + 127, 0) - down, 1)
    scale = np.exp2(byte - 127.0)
    codes = (blocks / scale).astype(np.float32).astype(dtype).astype(np.float64)
    return np.moveaxis((codes * scale).reshape(v.shape), -1, axis)


WIDE = False


def mx_kscale(k):
    if not WIDE:
        return np.ones(k)
    levels = np.array([10, -10, 5, -5, 0])
    if k % 512:
        return np.exp2(np.random.permutation(np.resize(levels, k // 32))).repeat(32)
    a = np.empty((k // 512, 16))
    for p in range(k // 512):
        a[p, :8] = np.random.permutation(np.resize(levels, 8))
        for g in range(8):
            far = levels[np.abs(levels - a[p, g]) >= 10]
            a[p, g + 8] = far[np.random.randint(len(far))]
    return np.exp2(a.ravel()).repeat(32)


def f64(x):
    return np.asarray(x).astype(np.float64)


def striped(idx):
    return np.tile(idx.reshape(-1, 16).T, (8, 1)).astype(np.uint16)


def unstriped(offs):
    return offs[:16].T.reshape(-1).astype(np.int64)


E2M1 = np.array([0.0, 0.5, 1.0, 1.5, 2.0, 3.0, 4.0, 6.0, -0.0, -0.5, -1.0, -1.5, -2.0, -3.0, -4.0, -6.0])


def pack_fp4(w):
    k, n = w.shape
    w = f64(np.asarray(w, np.float32).astype(ml_dtypes.bfloat16)).reshape(k // 32, 32, n)
    amax = np.abs(w).max(1)
    mant, ex = np.frexp(amax / 6.0)
    byte = np.clip(np.where(amax > 0, np.where(mant > 0.5, ex, ex - 1) + 127, 1), 1, 254)
    scaled = (w * np.exp2(127.0 - byte)[:, None, :]).reshape(k, n).astype(np.float32)
    c = np.ascontiguousarray(scaled.reshape(k // 512, 128, 4, n).transpose(0, 1, 3, 2)).astype(ml_dtypes.float4_e2m1fn).view(np.uint8) & 0xF
    words = (c[..., 0::2] | (c[..., 1::2] << 4)).reshape(k // 512, 128, 2 * n)
    return np.ascontiguousarray(words), np.ascontiguousarray(byte.astype(np.uint8).reshape(k // 512, 16, n))


def unpack_fp4(words, scales):
    g, _, n = scales.shape
    words = np.ascontiguousarray(words).reshape(g, 128, n, 2)
    nib = np.empty((g, 128, n, 4), np.uint8)
    nib[..., 0::2] = words & 0xF
    nib[..., 1::2] = words >> 4
    vals = E2M1[nib] * np.repeat(np.exp2(scales.astype(np.float64) - 127.0), 8, axis=1)[..., None]
    return vals.transpose(0, 1, 3, 2).reshape(g * 512, n)


def relu(v):
    return np.maximum(v, 0.0)


K, T, S, D, V, N = 1024, 2048, 1024, 3, 512, 128
P = 2 ** 7


def setup_inputs():
    n = np.random.standard_normal
    s = mx_kscale(K)[:, None]
    packed_xT = pack_fp4(n((K, T)) * s)
    return {
        "x_words": packed_xT[0],
        "x_scales": packed_xT[1],
        "w1": (n((K, N)) / np.sqrt(K) / s).astype(np.float32),
        "score": np.tile(np.random.standard_normal((D, 1, V)), (1, P, 1)).astype(np.float32),
        "offs": striped(np.random.permutation(T)[:S]),
        "pos1": striped(np.random.permutation(S)[:V]),
        "pos2": striped(np.random.permutation(S)[:V]),
        "pos3": striped(np.random.permutation(S)[:V]),
    }


def reference(x_words, x_scales, w1, score, offs, pos1, pos2, pos3):
    xq = unpack_fp4(x_words, x_scales)[:, unstriped(offs)]
    y = mxq(f64(w1), 0, "e4m3").T @ xq
    e0 = np.exp(f64(score)[0, :1])
    e1 = np.exp(f64(score)[1, :1])
    e2 = np.exp(f64(score)[2, :1])
    num = y[:, unstriped(pos1)] * e0 + y[:, unstriped(pos2)] * e1 + y[:, unstriped(pos3)] * e2
    den = e0 + e1 + e2
    return relu(num / den)

@@ -1,0 +1,186 @@
+from contextlib import ExitStack
+
+import concourse.mybir as mybir
+from concourse.masks import make_identity
+
+K, T, S, D, V, N = 1024, 2048, 1024, 3, 512, 128
+FLOPS = 2 * K * N * S
+
+F32 = mybir.dt.float32
+BF16 = mybir.dt.bfloat16
+I32 = mybir.dt.int32
+U32 = mybir.dt.uint32
+U16 = mybir.dt.uint16
+U8 = mybir.dt.uint8
+FP8X4 = mybir.dt.float8_e4m3fn_x4
+FP4X4 = mybir.dt.float4_e2m1fn_x4
+ALU = mybir.AluOpType
+ACT = mybir.ActivationFunctionType
+AXIS = mybir.AxisListType
+
+P = 128
+PACK = 4
+PASSES = K // (P * PACK)
+LIST_ROWS = 16
+SCALE_ROWS = 16
+
+
+def tile_picked_gatv_relu_p_kernel(
+    tc, x_words, x_scales, w1, score, offs, pos1, pos2, pos3, out
+):
+    nc = tc.nc
+    with ExitStack() as ctx:
+        keep = ctx.enter_context(tc.tile_pool(name="keep", bufs=1))
+        psum = ctx.enter_context(tc.psum_pool(name="psum", bufs=1))
+
+        offs_sb = keep.tile([P, S // LIST_ROWS], U16, name="offs_sb")
+        nc.sync.dma_start(offs_sb[:], offs)
+
+        first = P - PASSES * SCALE_ROWS
+        scale_table = keep.tile([P, T], U8, name="scale_table", align_bytes=64)
+        nc.sync.dma_start(
+            scale_table[first:P, :].bitcast(I32),
+            x_scales.rearrange("z q c -> (z q) c").bitcast(I32),
+        )
+        nc.vector.memset(scale_table[0:first, :].bitcast(I32), 0)
+
+        word_tables = [keep.tile([P, 2 * T], U8, name=f"word_table{z}", align_bytes=64) for z in range(PASSES)]
+        w_raw = keep.tile([P, PASSES, PACK, N], F32, name="w_raw", tag="w_raw", align_bytes=64)
+        nc.sync.dma_start(
+            w_raw[:].rearrange("p z j m -> p z (j m)"),
+            w1.rearrange("(z p j) m -> p z (j m)", z=PASSES, j=PACK),
+        )
+        for z in range(PASSES):
+            nc.sync.dma_start(word_tables[z][:].bitcast(I32), x_words[z].bitcast(I32))
+
+        scores = keep.tile([P, D, PACK], F32, name="scores")
+        nc.scalar.dma_start(scores[:], score[:, 0, :].rearrange("d (p j) -> p d j", j=PACK))
+        pos_sb = []
+        for d, pos in enumerate((pos1, pos2, pos3)):
+            tile = keep.tile([P, V // LIST_ROWS], U16, name=f"pos_sb{d}")
+            nc.sync.dma_start(tile[:], pos)
+            pos_sb.append(tile)
+
+        x_planes = [keep.tile([P, S], U8, name=f"x_plane{z}", align_bytes=64) for z in range(PASSES)]
+        for plane in x_planes:
+            nc.vector.memset(plane[:].bitcast(I32), 0)
+        ident = keep.tile([P, P], F32, name="ident")
+        make_identity(nc, ident[:])
+
+        low = keep.tile([P, PACK], F32, name="low")
+        expd = keep.tile([P, PACK, D], F32, name="expd")
+        den = keep.tile([P, PACK], F32, name="den")
+        att = keep.tile([P, PACK, D], F32, name="att")
+        by_target = keep.tile([P, PACK, D], F32, name="by_target")
+        nc.scalar.copy(by_target[:], scores[:].rearrange("p d j -> p j d"))
+        nc.vector.tensor_reduce(low[:], scores[:].rearrange("p d j -> p j d"), AXIS.X, ALU.max, negate=True)
+        for j in range(PACK):
+            nc.scalar.activation(
+                expd[:, j, :], by_target[:, j, :], ACT.Exp, bias=low[:, j : j + 1], accum_out=den[:, j : j + 1]
+            )
+
+        picked_scales = keep.tile([P, S], U8, name="picked_scales", align_bytes=64)
+        nc.vector.tensor_copy(picked_scales[:], scale_table[:].indirect(offs_sb[:]))
+        for z in range(PASSES):
+            for q in range(4):
+                row = first + SCALE_ROWS * z + 4 * q
+                nc.sync.dma_start(
+                    x_planes[z][32 * q : 32 * q + 4, :].bitcast(I32),
+                    picked_scales[row : row + 4, :].bitcast(I32),
+                )
+
+        inv = keep.tile([P, PACK], F32, name="inv")
+        nc.vector.reciprocal(inv[:], den[:])
+        for j in range(PACK):
+            nc.scalar.activation(att[:, j, :], expd[:, j, :], ACT.Copy, scale=inv[:, j : j + 1])
+
+        w_grouped = keep.tile([P, PASSES, N, PACK], BF16, name="w_grouped", align_bytes=64)
+        nc.scalar.copy(w_grouped[:], w_raw[:].rearrange("p z j m -> p z m j"))
+        w_codes = keep.tile([P, PASSES * N], U32, name="w_codes", align_bytes=64)
+        w_planes = keep.tile([P, PASSES * N], U8, name="w_planes", align_bytes=64)
+
+        def spread(d, tag):
+            bank = psum.tile([P, PACK, P], F32, name=f"att_bank{d}", tag=tag)
+            for j in range(PACK):
+                nc.tensor.transpose(bank[:, j, :], att[:, j, d : d + 1].to_broadcast([P, P]), ident[:])
+            rows = keep.tile([P, V], F32, name=f"att_rows{d}")
+            nc.scalar.copy(rows[:].rearrange("p (n j) -> p n j", j=PACK), bank[:].rearrange("p j n -> p n j"))
+            return rows
+
+        att_rows = [spread(0, "bank5"), spread(1, "bank6")]
+
+        gathers = [(0, 512), (512, 256), (768, 256)]
+        groups = [(0, 512), (512, 128), (640, 128), (768, 128), (896, 128)]
+        banks = [psum.tile([P, w], F32, name=f"y_bank{g}", tag=f"bank{g}") for g, (c0, w) in enumerate(groups)]
+        y = keep.tile([P, S], F32, name="y")
+        for z in range(PASSES):
+            cuts = [(0, 512), (512, 512)] if z == 0 else gathers
+            for c0, w in cuts:
+                if z == 0:
+                    picked = keep.tile([P, 2 * w], U8, name=f"picked{z}_{c0}", align_bytes=64)[:]
+                else:
+                    if c0 == 0:
+                        picked_all = keep.tile([P, 2 * S], U8, name="picked1", tag="w_raw", align_bytes=64)
+                    picked = picked_all[:, 2 * c0 : 2 * (c0 + w)]
+                nc.vector.tensor_copy(
+                    picked.bitcast(U16),
+                    word_tables[z][:].bitcast(U16).indirect(offs_sb[:, c0 // LIST_ROWS : (c0 + w) // LIST_ROWS]),
+                )
+                if z == 0 and c0 == 0:
+                    nc.vector.quantize_mx(
+                        out=w_codes[:].bitcast(FP8X4),
+                        scales=w_planes[:],
+                        in_=w_grouped[:].rearrange("p z m j -> p (z m j)"),
+                    )
+                for g, (g0, gw) in enumerate(groups):
+                    if c0 <= g0 < c0 + w:
+                        nc.tensor.matmul_mx(
+                            out=banks[g][:],
+                            lhsT=w_codes[:, z * N : (z + 1) * N].bitcast(FP8X4),
+                            lhsT_scale=w_planes[:, z * N : (z + 1) * N],
+                            rhs=picked[:, 2 * (g0 - c0) : 2 * (g0 - c0 + gw)].bitcast(FP4X4),
+                            rhs_scale=x_planes[z][:, g0 : g0 + gw],
+                            start=(z == 0),
+                            stop=(z == PASSES - 1),
+                        )
+                        if z == PASSES - 1:
+                            if g == len(groups) - 1:
+                                nc.vector.tensor_copy(y[:, g0 : g0 + gw], banks[g][:])
+                            else:
+                                nc.scalar.copy(y[:, g0 : g0 + gw], banks[g][:])
+
+        att_rows.append(spread(2, "bank4"))
+        terms = [keep.tile([P, V], F32, name=f"term{d}") for d in range(2)]
+        for d in range(2):
+            nc.vector.tensor_tensor(terms[d][:], y[:].indirect(pos_sb[d][:]), att_rows[d][:], ALU.mult)
+        pair = keep.tile([P, V], F32, name="pair")
+        pieces = [(0, 256), (256, 128), (384, 128)]
+        last = []
+
+        def fetch_last(c0, w):
+            term = keep.tile([P, w], F32, name=f"last{c0}")
+            nc.vector.tensor_tensor(
+                term[:],
+                y[:].indirect(pos_sb[2][:, c0 // LIST_ROWS : (c0 + w) // LIST_ROWS]),
+                att_rows[2][:, c0 : c0 + w],
+                ALU.mult,
+            )
+            last.append(term)
+
+        def finish(i):
+            c0, w = pieces[i]
+            total = keep.tile([P, w], F32, name=f"total{c0}")
+            nc.vector.tensor_tensor(total[:], pair[:, c0 : c0 + w], last[i][:], ALU.add)
+            result = keep.tile([P, w], F32, name=f"result{c0}")
+            if i == len(pieces) - 1:
+                nc.vector.tensor_scalar(result[:], total[:], 0.0, None, ALU.max)
+            else:
+                nc.scalar.activation(result[:], total[:], ACT.Relu)
+            nc.sync.dma_start(out[:, c0 : c0 + w], result[:])
+
+        fetch_last(*pieces[0])
+        nc.vector.tensor_tensor(pair[:], terms[0][:], terms[1][:], ALU.add)
+        for i in range(1, len(pieces)):
+            fetch_last(*pieces[i])
+            finish(i - 1)
+        finish(len(pieces) - 1)

@@ -71,7 +71,7 @@ def tile_picked_gatv_relu_p_kernel(
         expd = keep.tile([P, PACK, D], F32, name="expd")
         den = keep.tile([P, PACK], F32, name="den")
         att = keep.tile([P, PACK, D], F32, name="att")
-        by_target = keep.tile([P, PACK, D], F32, name="by_target")
+        by_target = keep.tile([P, PACK, D], F32, name="by_target", tag="w_grouped", align_bytes=64)
         nc.scalar.copy(by_target[:], scores[:].rearrange("p d j -> p j d"))
         nc.vector.tensor_reduce(low[:], scores[:].rearrange("p d j -> p j d"), AXIS.X, ALU.max, negate=True)
         for j in range(PACK):
@@ -94,7 +94,7 @@ def tile_picked_gatv_relu_p_kernel(
         for j in range(PACK):
             nc.scalar.activation(att[:, j, :], expd[:, j, :], ACT.Copy, scale=inv[:, j : j + 1])
 
-        w_grouped = keep.tile([P, PASSES, N, PACK], BF16, name="w_grouped", align_bytes=64)
+        w_grouped = keep.tile([P, PASSES, N, PACK], BF16, name="w_grouped", tag="w_grouped", align_bytes=64)
         nc.scalar.copy(w_grouped[:], w_raw[:].rearrange("p z j m -> p z m j"))
         w_codes = keep.tile([P, PASSES * N], U32, name="w_codes", align_bytes=64)
         w_planes = keep.tile([P, PASSES * N], U8, name="w_planes", align_bytes=64)
@@ -107,7 +107,7 @@ def tile_picked_gatv_relu_p_kernel(
             nc.scalar.copy(rows[:].rearrange("p (n j) -> p n j", j=PACK), bank[:].rearrange("p j n -> p n j"))
             return rows
 
-        att_rows = [spread(0, "bank5"), spread(1, "bank6")]
+        att_rows = [spread(d, f"bank{5 + d}") for d in range(D)]
 
         gathers = [(0, 512), (512, 256), (768, 256)]
         groups = [(0, 512), (512, 128), (640, 128), (768, 128), (896, 128)]
@@ -116,12 +116,9 @@ def tile_picked_gatv_relu_p_kernel(
         for z in range(PASSES):
             cuts = [(0, 512), (512, 512)] if z == 0 else gathers
             for c0, w in cuts:
-                if z == 0:
-                    picked = keep.tile([P, 2 * w], U8, name=f"picked{z}_{c0}", align_bytes=64)[:]
-                else:
-                    if c0 == 0:
-                        picked_all = keep.tile([P, 2 * S], U8, name="picked1", tag="w_raw", align_bytes=64)
-                    picked = picked_all[:, 2 * c0 : 2 * (c0 + w)]
+                if c0 == 0:
+                    picked_all = keep.tile([P, 2 * S], U8, name=f"picked{z}", tag=("w_raw", "w_grouped")[z], align_bytes=64)
+                picked = picked_all[:, 2 * c0 : 2 * (c0 + w)]
                 nc.vector.tensor_copy(
                     picked.bitcast(U16),
                     word_tables[z][:].bitcast(U16).indirect(offs_sb[:, c0 // LIST_ROWS : (c0 + w) // LIST_ROWS]),
@@ -149,38 +146,45 @@ def tile_picked_gatv_relu_p_kernel(
                             else:
                                 nc.scalar.copy(y[:, g0 : g0 + gw], banks[g][:])
 
-        att_rows.append(spread(2, "bank4"))
-        terms = [keep.tile([P, V], F32, name=f"term{d}") for d in range(2)]
-        for d in range(2):
-            nc.vector.tensor_tensor(terms[d][:], y[:].indirect(pos_sb[d][:]), att_rows[d][:], ALU.mult)
-        pair = keep.tile([P, V], F32, name="pair")
-        pieces = [(0, 256), (256, 128), (384, 128)]
-        last = []
 
-        def fetch_last(c0, w):
-            term = keep.tile([P, w], F32, name=f"last{c0}")
+        def fetch(d, c0, w):
+            term = keep.tile([P, w], F32, name=f"term{d}_{c0}")
             nc.vector.tensor_tensor(
                 term[:],
-                y[:].indirect(pos_sb[2][:, c0 // LIST_ROWS : (c0 + w) // LIST_ROWS]),
-                att_rows[2][:, c0 : c0 + w],
+                y[:].indirect(pos_sb[d][:, c0 // LIST_ROWS : (c0 + w) // LIST_ROWS]),
+                att_rows[d][:, c0 : c0 + w],
                 ALU.mult,
             )
-            last.append(term)
+            return term
 
-        def finish(i):
-            c0, w = pieces[i]
-            total = keep.tile([P, w], F32, name=f"total{c0}")
-            nc.vector.tensor_tensor(total[:], pair[:, c0 : c0 + w], last[i][:], ALU.add)
-            result = keep.tile([P, w], F32, name=f"result{c0}")
-            if i == len(pieces) - 1:
+        half = V // 2
+        sums = [psum.tile([P, P], F32, name=f"sum{i}", tag=f"bank{i}") for i in range(2)]
+        for d in range(D):
+            term = fetch(d, 0, half)
+            for i in range(2):
+                nc.tensor.matmul(
+                    sums[i][:], term[:, i * P : (i + 1) * P], ident[:], start=(d == 0), stop=(d == D - 1), is_transpose=True
+                )
+        early = keep.tile([P, half], F32, name="early")
+        for i in range(2):
+            turned = keep.tile([P, P], F32, name=f"turned{i}")
+            nc.scalar.activation(turned[:], sums[i][:], ACT.Relu)
+            back = psum.tile([P, P], F32, name=f"back{i}", tag=f"bank{2 + i}")
+            nc.tensor.transpose(back[:], turned[:], ident[:])
+            nc.scalar.copy(early[:, i * P : (i + 1) * P], back[:])
+        nc.sync.dma_start(out[:, 0:half], early[:])
+
+        terms = [fetch(d, half, half) for d in range(2)]
+        last = [fetch(2, half, P)]
+        pair = keep.tile([P, half], F32, name="pair")
+        nc.vector.tensor_tensor(pair[:], terms[0][:], terms[1][:], ALU.add)
+        last.append(fetch(2, half + P, P))
+        for i in range(2):
+            total = keep.tile([P, P], F32, name=f"total{i}")
+            nc.vector.tensor_tensor(total[:], pair[:, i * P : (i + 1) * P], last[i][:], ALU.add)
+            result = keep.tile([P, P], F32, name=f"result{i}")
+            if i == 1:
                 nc.vector.tensor_scalar(result[:], total[:], 0.0, None, ALU.max)
             else:
                 nc.scalar.activation(result[:], total[:], ACT.Relu)
-            nc.sync.dma_start(out[:, c0 : c0 + w], result[:])
-
-        fetch_last(*pieces[0])
-        nc.vector.tensor_tensor(pair[:], terms[0][:], terms[1][:], ALU.add)
-        for i in range(1, len(pieces)):
-            fetch_last(*pieces[i])
-            finish(i - 1)
-        finish(len(pieces) - 1)
+            nc.sync.dma_start(out[:, half + i * P : half + (i + 1) * P], result[:])

@@ -23,6 +23,7 @@ PACK = 4
 PASSES = K // (P * PACK)
 LIST_ROWS = 16
 SCALE_ROWS = 16
+BLOCKS = V // P
 
 
 def tile_picked_gatv_relu_p_kernel(
@@ -44,17 +45,21 @@ def tile_picked_gatv_relu_p_kernel(
         )
         nc.vector.memset(scale_table[0:first, :].bitcast(I32), 0)
 
-        word_tables = [keep.tile([P, 2 * T], U8, name=f"word_table{z}", align_bytes=64) for z in range(PASSES)]
-        w_raw = keep.tile([P, PASSES, PACK, N], F32, name="w_raw", tag="w_raw", align_bytes=64)
-        nc.sync.dma_start(
-            w_raw[:].rearrange("p z j m -> p z (j m)"),
-            w1.rearrange("(z p j) m -> p z (j m)", z=PASSES, j=PACK),
-        )
-        for z in range(PASSES):
-            nc.sync.dma_start(word_tables[z][:].bitcast(I32), x_words[z].bitcast(I32))
+        live = P - BLOCKS
+        score_rows = keep.tile([P, D, P], F32, name="score_rows", tag="score_rows", align_bytes=64)
+        nc.sync.dma_start(score_rows[live:P], score[:, 0, :].rearrange("d (b n) -> b d n", n=P))
+        nc.gpsimd.memset(score_rows[0:96], 0.0)
+        nc.gpsimd.memset(score_rows[96:live], 0.0)
 
-        scores = keep.tile([P, D, PACK], F32, name="scores")
-        nc.scalar.dma_start(scores[:], score[:, 0, :].rearrange("d (p j) -> p d j", j=PACK))
+        word_tables, w_raw = [], []
+        for z in range(PASSES):
+            rows = keep.tile([P, PACK, N], F32, name=f"w_raw{z}", tag=f"w_raw{z}", align_bytes=64)
+            nc.sync.dma_start(rows[:], w1[z * P * PACK : (z + 1) * P * PACK, :].rearrange("(p j) m -> p j m", j=PACK))
+            w_raw.append(rows)
+            table = keep.tile([P, 2 * T], U8, name=f"word_table{z}", align_bytes=64)
+            nc.sync.dma_start(table[:].bitcast(I32), x_words[z].bitcast(I32))
+            word_tables.append(table)
+
         pos_sb = []
         for d, pos in enumerate((pos1, pos2, pos3)):
             tile = keep.tile([P, V // LIST_ROWS], U16, name=f"pos_sb{d}")
@@ -67,18 +72,6 @@ def tile_picked_gatv_relu_p_kernel(
         ident = keep.tile([P, P], F32, name="ident")
         make_identity(nc, ident[:])
 
-        low = keep.tile([P, PACK], F32, name="low")
-        expd = keep.tile([P, PACK, D], F32, name="expd")
-        den = keep.tile([P, PACK], F32, name="den")
-        att = keep.tile([P, PACK, D], F32, name="att")
-        by_target = keep.tile([P, PACK, D], F32, name="by_target", tag="w_grouped", align_bytes=64)
-        nc.scalar.copy(by_target[:], scores[:].rearrange("p d j -> p j d"))
-        nc.vector.tensor_reduce(low[:], scores[:].rearrange("p d j -> p j d"), AXIS.X, ALU.max, negate=True)
-        for j in range(PACK):
-            nc.scalar.activation(
-                expd[:, j, :], by_target[:, j, :], ACT.Exp, bias=low[:, j : j + 1], accum_out=den[:, j : j + 1]
-            )
-
         picked_scales = keep.tile([P, S], U8, name="picked_scales", align_bytes=64)
         nc.vector.tensor_copy(picked_scales[:], scale_table[:].indirect(offs_sb[:]))
         for z in range(PASSES):
@@ -89,52 +82,74 @@ def tile_picked_gatv_relu_p_kernel(
                     picked_scales[row : row + 4, :].bitcast(I32),
                 )
 
-        inv = keep.tile([P, PACK], F32, name="inv")
-        nc.vector.reciprocal(inv[:], den[:])
-        for j in range(PACK):
-            nc.scalar.activation(att[:, j, :], expd[:, j, :], ACT.Copy, scale=inv[:, j : j + 1])
+        def cast(z):
+            grouped = keep.tile([P, N, PACK], BF16, name=f"w_grouped{z}", tag=f"w_grouped{z}", align_bytes=64)
+            nc.scalar.copy(grouped[:], w_raw[z][:].rearrange("p j m -> p m j"))
+            return grouped
 
-        w_grouped = keep.tile([P, PASSES, N, PACK], BF16, name="w_grouped", tag="w_grouped", align_bytes=64)
-        nc.scalar.copy(w_grouped[:], w_raw[:].rearrange("p z j m -> p z m j"))
-        w_codes = keep.tile([P, PASSES * N], U32, name="w_codes", align_bytes=64)
-        w_planes = keep.tile([P, PASSES * N], U8, name="w_planes", align_bytes=64)
+        def quantise(z, grouped):
+            codes = keep.tile([P, N], U32, name=f"w_codes{z}", align_bytes=64)
+            plane = keep.tile([P, N], U8, name=f"w_plane{z}", align_bytes=64)
+            nc.vector.quantize_mx(
+                out=codes[:].bitcast(FP8X4), scales=plane[:], in_=grouped[:].rearrange("p m j -> p (m j)")
+            )
+            return codes, plane
+
+        weights = [quantise(0, cast(0))]
+
+        score_bank = psum.tile([P, D, P], F32, name="score_bank", tag="bank7")
+        for d in range(D):
+            nc.tensor.transpose(score_bank[:, d, :], score_rows[:, d, :], ident[:])
+        low = keep.tile([P, BLOCKS], F32, name="low", tag="w_grouped1", align_bytes=64)
+        expd = keep.tile([P, BLOCKS, D], F32, name="expd", tag="w_raw0", align_bytes=64)
+        den = keep.tile([P, BLOCKS], F32, name="den")
+        inv = keep.tile([P, BLOCKS], F32, name="inv")
+        att = keep.tile([P, BLOCKS, D], F32, name="att")
+        nc.vector.tensor_reduce(
+            low[:], score_bank[:, :, live:P].rearrange("p d b -> p b d"), AXIS.X, ALU.max, negate=True
+        )
+        for b in range(BLOCKS):
+            nc.scalar.activation(
+                expd[:, b, :], score_bank[:, :, live + b], ACT.Exp, bias=low[:, b : b + 1], accum_out=den[:, b : b + 1]
+            )
+        nc.vector.reciprocal(inv[:], den[:])
+        for b in range(BLOCKS):
+            nc.scalar.activation(att[:, b, :], expd[:, b, :], ACT.Copy, scale=inv[:, b : b + 1])
 
         def spread(d, tag):
-            bank = psum.tile([P, PACK, P], F32, name=f"att_bank{d}", tag=tag)
-            for j in range(PACK):
-                nc.tensor.transpose(bank[:, j, :], att[:, j, d : d + 1].to_broadcast([P, P]), ident[:])
+            bank = psum.tile([P, V], F32, name=f"att_bank{d}", tag=tag)
+            for b in range(BLOCKS):
+                nc.tensor.transpose(bank[:, b * P : (b + 1) * P], att[:, b, d : d + 1].to_broadcast([P, P]), ident[:])
             rows = keep.tile([P, V], F32, name=f"att_rows{d}")
-            nc.scalar.copy(rows[:].rearrange("p (n j) -> p n j", j=PACK), bank[:].rearrange("p j n -> p n j"))
+            nc.scalar.copy(rows[:], bank[:])
             return rows
 
-        att_rows = [spread(d, f"bank{5 + d}") for d in range(D)]
+        att_rows = [spread(0, "bank5"), spread(1, "bank6")]
+        weights.append(quantise(1, cast(1)))
 
-        gathers = [(0, 512), (512, 256), (768, 256)]
         groups = [(0, 512), (512, 128), (640, 128), (768, 128), (896, 128)]
         banks = [psum.tile([P, w], F32, name=f"y_bank{g}", tag=f"bank{g}") for g, (c0, w) in enumerate(groups)]
         y = keep.tile([P, S], F32, name="y")
+        cuts = [[(0, 512), (512, 512)], [(0, 512), (512, 256), (768, 256)]]
         for z in range(PASSES):
-            cuts = [(0, 512), (512, 512)] if z == 0 else gathers
-            for c0, w in cuts:
-                if c0 == 0:
-                    picked_all = keep.tile([P, 2 * S], U8, name=f"picked{z}", tag=("w_raw", "w_grouped")[z], align_bytes=64)
-                picked = picked_all[:, 2 * c0 : 2 * (c0 + w)]
+            codes, plane = weights[z]
+            for c0, w in cuts[z]:
+                if z == 0:
+                    picked = keep.tile([P, 2 * w], U8, name=f"picked0_{c0}", tag="w_raw1" if c0 else "score_rows", align_bytes=64)[:]
+                else:
+                    if c0 == 0:
+                        picked_all = keep.tile([P, 2 * S], U8, name="picked1", tag="w_grouped1", align_bytes=64)
+                    picked = picked_all[:, 2 * c0 : 2 * (c0 + w)]
                 nc.vector.tensor_copy(
                     picked.bitcast(U16),
                     word_tables[z][:].bitcast(U16).indirect(offs_sb[:, c0 // LIST_ROWS : (c0 + w) // LIST_ROWS]),
                 )
-                if z == 0 and c0 == 0:
-                    nc.vector.quantize_mx(
-                        out=w_codes[:].bitcast(FP8X4),
-                        scales=w_planes[:],
-                        in_=w_grouped[:].rearrange("p z m j -> p (z m j)"),
-                    )
                 for g, (g0, gw) in enumerate(groups):
                     if c0 <= g0 < c0 + w:
                         nc.tensor.matmul_mx(
                             out=banks[g][:],
-                            lhsT=w_codes[:, z * N : (z + 1) * N].bitcast(FP8X4),
-                            lhsT_scale=w_planes[:, z * N : (z + 1) * N],
+                            lhsT=codes[:].bitcast(FP8X4),
+                            lhsT_scale=plane[:],
                             rhs=picked[:, 2 * (g0 - c0) : 2 * (g0 - c0 + gw)].bitcast(FP4X4),
                             rhs_scale=x_planes[z][:, g0 : g0 + gw],
                             start=(z == 0),
@@ -146,45 +161,38 @@ def tile_picked_gatv_relu_p_kernel(
                             else:
                                 nc.scalar.copy(y[:, g0 : g0 + gw], banks[g][:])
 
+        att_rows.append(spread(2, "bank4"))
+        terms = [keep.tile([P, V], F32, name=f"term{d}") for d in range(2)]
+        for d in range(2):
+            nc.vector.tensor_tensor(terms[d][:], y[:].indirect(pos_sb[d][:]), att_rows[d][:], ALU.mult)
+        pair = keep.tile([P, V], F32, name="pair")
+        pieces = [(0, 256), (256, 128), (384, 128)]
+        last = []
 
-        def fetch(d, c0, w):
-            term = keep.tile([P, w], F32, name=f"term{d}_{c0}")
+        def fetch_last(c0, w):
+            term = keep.tile([P, w], F32, name=f"last{c0}")
             nc.vector.tensor_tensor(
                 term[:],
-                y[:].indirect(pos_sb[d][:, c0 // LIST_ROWS : (c0 + w) // LIST_ROWS]),
-                att_rows[d][:, c0 : c0 + w],
+                y[:].indirect(pos_sb[2][:, c0 // LIST_ROWS : (c0 + w) // LIST_ROWS]),
+                att_rows[2][:, c0 : c0 + w],
                 ALU.mult,
             )
-            return term
+            last.append(term)
 
-        half = V // 2
-        sums = [psum.tile([P, P], F32, name=f"sum{i}", tag=f"bank{i}") for i in range(2)]
-        for d in range(D):
-            term = fetch(d, 0, half)
-            for i in range(2):
-                nc.tensor.matmul(
-                    sums[i][:], term[:, i * P : (i + 1) * P], ident[:], start=(d == 0), stop=(d == D - 1), is_transpose=True
-                )
-        early = keep.tile([P, half], F32, name="early")
-        for i in range(2):
-            turned = keep.tile([P, P], F32, name=f"turned{i}")
-            nc.scalar.activation(turned[:], sums[i][:], ACT.Relu)
-            back = psum.tile([P, P], F32, name=f"back{i}", tag=f"bank{2 + i}")
-            nc.tensor.transpose(back[:], turned[:], ident[:])
-            nc.scalar.copy(early[:, i * P : (i + 1) * P], back[:])
-        nc.sync.dma_start(out[:, 0:half], early[:])
-
-        terms = [fetch(d, half, half) for d in range(2)]
-        last = [fetch(2, half, P)]
-        pair = keep.tile([P, half], F32, name="pair")
-        nc.vector.tensor_tensor(pair[:], terms[0][:], terms[1][:], ALU.add)
-        last.append(fetch(2, half + P, P))
-        for i in range(2):
-            total = keep.tile([P, P], F32, name=f"total{i}")
-            nc.vector.tensor_tensor(total[:], pair[:, i * P : (i + 1) * P], last[i][:], ALU.add)
-            result = keep.tile([P, P], F32, name=f"result{i}")
-            if i == 1:
+        def finish(i):
+            c0, w = pieces[i]
+            total = keep.tile([P, w], F32, name=f"total{c0}")
+            nc.vector.tensor_tensor(total[:], pair[:, c0 : c0 + w], last[i][:], ALU.add)
+            result = keep.tile([P, w], F32, name=f"result{c0}")
+            if i == len(pieces) - 1:
                 nc.vector.tensor_scalar(result[:], total[:], 0.0, None, ALU.max)
             else:
                 nc.scalar.activation(result[:], total[:], ACT.Relu)
-            nc.sync.dma_start(out[:, half + i * P : half + (i + 1) * P], result[:])
+            nc.sync.dma_start(out[:, c0 : c0 + w], result[:])
+
+        fetch_last(*pieces[0])
+        nc.vector.tensor_tensor(pair[:], terms[0][:], terms[1][:], ALU.add)
+        for i in range(1, len(pieces)):
+            fetch_last(*pieces[i])
+            finish(i - 1)
+        finish(len(pieces) - 1)

@@ -41,7 +41,7 @@ def tile_picked_gatv_relu_p_kernel(
         scale_table = keep.tile([P, T], U8, name="scale_table", align_bytes=64)
         nc.sync.dma_start(
             scale_table[first:P, :].bitcast(I32),
-            x_scales.rearrange("z q c -> (z q) c").bitcast(I32),
+            x_scales.rearrange("z q c -> q z c").bitcast(I32),
         )
         nc.vector.memset(scale_table[0:first, :].bitcast(I32), 0)
 
@@ -56,7 +56,8 @@ def tile_picked_gatv_relu_p_kernel(
             rows = keep.tile([P, PACK, N], F32, name=f"w_raw{z}", tag=f"w_raw{z}", align_bytes=64)
             nc.sync.dma_start(rows[:], w1[z * P * PACK : (z + 1) * P * PACK, :].rearrange("(p j) m -> p j m", j=PACK))
             w_raw.append(rows)
-            table = keep.tile([P, 2 * T], U8, name=f"word_table{z}", align_bytes=64)
+        for z in range(PASSES):
+            table = keep.tile([P, 2 * T], U8, name=f"word_table{z}", tag=f"word_table{z}", align_bytes=64)
             nc.sync.dma_start(table[:].bitcast(I32), x_words[z].bitcast(I32))
             word_tables.append(table)
 
@@ -66,21 +67,19 @@ def tile_picked_gatv_relu_p_kernel(
             nc.sync.dma_start(tile[:], pos)
             pos_sb.append(tile)
 
-        x_planes = [keep.tile([P, S], U8, name=f"x_plane{z}", align_bytes=64) for z in range(PASSES)]
-        for plane in x_planes:
-            nc.vector.memset(plane[:].bitcast(I32), 0)
+        x_planes = keep.tile([P, PASSES * S], U8, name="x_planes", align_bytes=64)
+        nc.vector.memset(x_planes[:].bitcast(I32), 0)
         ident = keep.tile([P, P], F32, name="ident")
         make_identity(nc, ident[:])
 
         picked_scales = keep.tile([P, S], U8, name="picked_scales", align_bytes=64)
         nc.vector.tensor_copy(picked_scales[:], scale_table[:].indirect(offs_sb[:]))
-        for z in range(PASSES):
-            for q in range(4):
-                row = first + SCALE_ROWS * z + 4 * q
-                nc.sync.dma_start(
-                    x_planes[z][32 * q : 32 * q + 4, :].bitcast(I32),
-                    picked_scales[row : row + 4, :].bitcast(I32),
-                )
+        for q in range(4):
+            row = first + 8 * q
+            nc.sync.dma_start(
+                x_planes[32 * q : 32 * q + 4, :].bitcast(I32),
+                picked_scales[row : row + 8, :].bitcast(I32),
+            )
 
         def cast(z):
             grouped = keep.tile([P, N, PACK], BF16, name=f"w_grouped{z}", tag=f"w_grouped{z}", align_bytes=64)
@@ -95,16 +94,14 @@ def tile_picked_gatv_relu_p_kernel(
             )
             return codes, plane
 
-        weights = [quantise(0, cast(0))]
+        weights = [quantise(z, cast(z)) for z in range(PASSES)]
 
         score_bank = psum.tile([P, D, P], F32, name="score_bank", tag="bank7")
         for d in range(D):
             nc.tensor.transpose(score_bank[:, d, :], score_rows[:, d, :], ident[:])
-        low = keep.tile([P, BLOCKS], F32, name="low", tag="w_grouped1", align_bytes=64)
-        expd = keep.tile([P, BLOCKS, D], F32, name="expd", tag="w_raw0", align_bytes=64)
+        low = keep.tile([P, BLOCKS], F32, name="low")
+        expd = keep.tile([P, BLOCKS, D], F32, name="expd")
         den = keep.tile([P, BLOCKS], F32, name="den")
-        inv = keep.tile([P, BLOCKS], F32, name="inv")
-        att = keep.tile([P, BLOCKS, D], F32, name="att")
         nc.vector.tensor_reduce(
             low[:], score_bank[:, :, live:P].rearrange("p d b -> p b d"), AXIS.X, ALU.max, negate=True
         )
@@ -112,87 +109,96 @@ def tile_picked_gatv_relu_p_kernel(
             nc.scalar.activation(
                 expd[:, b, :], score_bank[:, :, live + b], ACT.Exp, bias=low[:, b : b + 1], accum_out=den[:, b : b + 1]
             )
-        nc.vector.reciprocal(inv[:], den[:])
-        for b in range(BLOCKS):
-            nc.scalar.activation(att[:, b, :], expd[:, b, :], ACT.Copy, scale=inv[:, b : b + 1])
 
-        def spread(d, tag):
-            bank = psum.tile([P, V], F32, name=f"att_bank{d}", tag=tag)
-            for b in range(BLOCKS):
-                nc.tensor.transpose(bank[:, b * P : (b + 1) * P], att[:, b, d : d + 1].to_broadcast([P, P]), ident[:])
-            rows = keep.tile([P, V], F32, name=f"att_rows{d}")
+        half = V // 2
+        turned_blocks = half // P
+
+        def spread(first_d, count, tag):
+            bank = psum.tile([P, count, half], F32, name=f"att_bank{first_d}", tag=tag)
+            for i in range(count):
+                for b in range(turned_blocks, BLOCKS):
+                    c0 = (b - turned_blocks) * P
+                    nc.tensor.transpose(
+                        bank[:, i, c0 : c0 + P], att[:, b, first_d + i : first_d + i + 1].to_broadcast([P, P]), ident[:]
+                    )
+            rows = keep.tile([P, count, half], F32, name=f"att_rows{first_d}")
             nc.scalar.copy(rows[:], bank[:])
-            return rows
+            return [rows[:, i, :] for i in range(count)]
 
-        att_rows = [spread(0, "bank5"), spread(1, "bank6")]
-        weights.append(quantise(1, cast(1)))
 
         groups = [(0, 512), (512, 128), (640, 128), (768, 128), (896, 128)]
         banks = [psum.tile([P, w], F32, name=f"y_bank{g}", tag=f"bank{g}") for g, (c0, w) in enumerate(groups)]
         y = keep.tile([P, S], F32, name="y")
-        cuts = [[(0, 512), (512, 512)], [(0, 512), (512, 256), (768, 256)]]
-        for z in range(PASSES):
+        steps = [(0, 0, 512), (0, 512, 512), (1, 0, 512), (1, 512, 256), (1, 768, 256)]
+        seen = set()
+        for z, c0, w in steps:
             codes, plane = weights[z]
-            for c0, w in cuts[z]:
-                if z == 0:
-                    picked = keep.tile([P, 2 * w], U8, name=f"picked0_{c0}", tag="w_raw1" if c0 else "score_rows", align_bytes=64)[:]
-                else:
-                    if c0 == 0:
-                        picked_all = keep.tile([P, 2 * S], U8, name="picked1", tag="w_grouped1", align_bytes=64)
-                    picked = picked_all[:, 2 * c0 : 2 * (c0 + w)]
-                nc.vector.tensor_copy(
-                    picked.bitcast(U16),
-                    word_tables[z][:].bitcast(U16).indirect(offs_sb[:, c0 // LIST_ROWS : (c0 + w) // LIST_ROWS]),
-                )
-                for g, (g0, gw) in enumerate(groups):
-                    if c0 <= g0 < c0 + w:
-                        nc.tensor.matmul_mx(
-                            out=banks[g][:],
-                            lhsT=codes[:].bitcast(FP8X4),
-                            lhsT_scale=plane[:],
-                            rhs=picked[:, 2 * (g0 - c0) : 2 * (g0 - c0 + gw)].bitcast(FP4X4),
-                            rhs_scale=x_planes[z][:, g0 : g0 + gw],
-                            start=(z == 0),
-                            stop=(z == PASSES - 1),
-                        )
-                        if z == PASSES - 1:
-                            if g == len(groups) - 1:
-                                nc.vector.tensor_copy(y[:, g0 : g0 + gw], banks[g][:])
-                            else:
-                                nc.scalar.copy(y[:, g0 : g0 + gw], banks[g][:])
+            picked = keep.tile([P, 2 * w], U8, name=f"picked{z}_{c0}", tag=f"picked{z}_{c0}", align_bytes=64)[:]
+            nc.vector.tensor_copy(
+                picked.bitcast(U16),
+                word_tables[z][:].bitcast(U16).indirect(offs_sb[:, c0 // LIST_ROWS : (c0 + w) // LIST_ROWS]),
+            )
+            for g, (g0, gw) in enumerate(groups):
+                if c0 <= g0 < c0 + w:
+                    closing = g in seen
+                    seen.add(g)
+                    nc.tensor.matmul_mx(
+                        out=banks[g][:],
+                        lhsT=codes[:].bitcast(FP8X4),
+                        lhsT_scale=plane[:],
+                        rhs=picked[:, 2 * (g0 - c0) : 2 * (g0 - c0 + gw)].bitcast(FP4X4),
+                        rhs_scale=x_planes[:, z * S + g0 : z * S + g0 + gw],
+                        start=not closing,
+                        stop=closing,
+                    )
+                    if closing and g in (1, 2, 3):
+                        nc.vector.tensor_copy(y[:, g0 : g0 + gw], banks[g][:])
+                    elif closing:
+                        nc.scalar.copy(y[:, g0 : g0 + gw], banks[g][:])
 
-        att_rows.append(spread(2, "bank4"))
-        terms = [keep.tile([P, V], F32, name=f"term{d}") for d in range(2)]
-        for d in range(2):
-            nc.vector.tensor_tensor(terms[d][:], y[:].indirect(pos_sb[d][:]), att_rows[d][:], ALU.mult)
-        pair = keep.tile([P, V], F32, name="pair")
-        pieces = [(0, 256), (256, 128), (384, 128)]
-        last = []
+        inv = keep.tile([P, BLOCKS], F32, name="inv", tag="word_table1", align_bytes=64)
+        att = keep.tile([P, BLOCKS, D], F32, name="att", tag="picked1_512", align_bytes=64)
+        nc.vector.reciprocal(inv[:], den[:])
+        nc.vector.tensor_tensor(att[:], expd[:], inv[:].unsqueeze(2).to_broadcast([P, BLOCKS, D]), ALU.mult)
+        att_rows = spread(0, 2, "bank1") + spread(2, 1, "bank2")
 
-        def fetch_last(c0, w):
-            term = keep.tile([P, w], F32, name=f"last{c0}")
+        sums = [psum.tile([P, P], F32, name=f"sum{b}", tag=f"bank{3 + b}") for b in range(turned_blocks)]
+        for d in range(D):
+            fetched = keep.tile([P, half], F32, name=f"fetched{d}")
+            nc.vector.tensor_copy(fetched[:], y[:].indirect(pos_sb[d][:, 0 : half // LIST_ROWS]))
+            turned = psum.tile([P, turned_blocks, P], F32, name=f"turned{d}", tag=f"bank{5 + d}")
+            for b in range(turned_blocks):
+                nc.tensor.transpose(turned[:, b, :], fetched[:, b * P : (b + 1) * P], ident[:])
+            for b in range(turned_blocks):
+                weighted = keep.tile([P, P], F32, name=f"weighted{d}_{b}")
+                nc.scalar.activation(weighted[:], turned[:, b, :], ACT.Copy, scale=att[:, b, d : d + 1])
+                nc.tensor.matmul(sums[b][:], weighted[:], ident[:], start=(d == 0), stop=(d == D - 1), is_transpose=True)
+        low_result = keep.tile([P, half], F32, name="low_result")
+        for b in range(turned_blocks):
+            nc.scalar.activation(low_result[:, b * P : (b + 1) * P], sums[b][:], ACT.Relu)
+        nc.sync.dma_start(out[:, 0:half], low_result[:])
+
+        def fetch(d, c0, w):
+            term = keep.tile([P, w], F32, name=f"term{d}_{c0}")
             nc.vector.tensor_tensor(
                 term[:],
-                y[:].indirect(pos_sb[2][:, c0 // LIST_ROWS : (c0 + w) // LIST_ROWS]),
-                att_rows[2][:, c0 : c0 + w],
+                y[:].indirect(pos_sb[d][:, (half + c0) // LIST_ROWS : (half + c0 + w) // LIST_ROWS]),
+                att_rows[d][:, c0 : c0 + w],
                 ALU.mult,
             )
-            last.append(term)
+            return term
 
-        def finish(i):
-            c0, w = pieces[i]
-            total = keep.tile([P, w], F32, name=f"total{c0}")
-            nc.vector.tensor_tensor(total[:], pair[:, c0 : c0 + w], last[i][:], ALU.add)
-            result = keep.tile([P, w], F32, name=f"result{c0}")
-            if i == len(pieces) - 1:
-                nc.vector.tensor_scalar(result[:], total[:], 0.0, None, ALU.max)
-            else:
-                nc.scalar.activation(result[:], total[:], ACT.Relu)
-            nc.sync.dma_start(out[:, c0 : c0 + w], result[:])
-
-        fetch_last(*pieces[0])
+        terms = [fetch(d, 0, half) for d in range(2)]
+        last = [fetch(2, 0, P)]
+        pair = keep.tile([P, half], F32, name="pair")
         nc.vector.tensor_tensor(pair[:], terms[0][:], terms[1][:], ALU.add)
-        for i in range(1, len(pieces)):
-            fetch_last(*pieces[i])
-            finish(i - 1)
-        finish(len(pieces) - 1)
+        last.append(fetch(2, P, P))
+        totals = []
+        for i in range(2):
+            total = keep.tile([P, P], F32, name=f"total{i}")
+            nc.vector.tensor_tensor(total[:], pair[:, i * P : (i + 1) * P], last[i][:], ALU.add)
+            totals.append(total)
+        for i in range(2):
+            result = keep.tile([P, P], F32, name=f"result{i}")
+            nc.vector.tensor_scalar(result[:], totals[i][:], 0.0, None, ALU.max)
+            nc.sync.dma_start(out[:, half + i * P : half + (i + 1) * P], result[:])

@@ -67,19 +67,24 @@ def tile_picked_gatv_relu_p_kernel(
             nc.sync.dma_start(tile[:], pos)
             pos_sb.append(tile)
 
-        x_planes = keep.tile([P, PASSES * S], U8, name="x_planes", align_bytes=64)
-        nc.vector.memset(x_planes[:].bitcast(I32), 0)
+        wide = S // 2
+        x_planes = [keep.tile([P, PASSES * wide], U8, name=f"x_planes{h}", align_bytes=64) for h in range(2)]
+        for planes in x_planes:
+            nc.vector.memset(planes[:].bitcast(I32), 0)
         ident = keep.tile([P, P], F32, name="ident")
         make_identity(nc, ident[:])
 
-        picked_scales = keep.tile([P, S], U8, name="picked_scales", align_bytes=64)
-        nc.vector.tensor_copy(picked_scales[:], scale_table[:].indirect(offs_sb[:]))
-        for q in range(4):
-            row = first + 8 * q
-            nc.sync.dma_start(
-                x_planes[32 * q : 32 * q + 4, :].bitcast(I32),
-                picked_scales[row : row + 8, :].bitcast(I32),
+        for h in range(2):
+            picked_scales = keep.tile([P, wide], U8, name=f"picked_scales{h}", align_bytes=64)
+            nc.vector.tensor_copy(
+                picked_scales[:], scale_table[:].indirect(offs_sb[:, h * wide // LIST_ROWS : (h + 1) * wide // LIST_ROWS])
             )
+            for q in range(4):
+                row = first + 8 * q
+                nc.sync.dma_start(
+                    x_planes[h][32 * q : 32 * q + 4, :].bitcast(I32),
+                    picked_scales[row : row + 8, :].bitcast(I32),
+                )
 
         def cast(z):
             grouped = keep.tile([P, N, PACK], BF16, name=f"w_grouped{z}", tag=f"w_grouped{z}", align_bytes=64)
@@ -133,7 +138,7 @@ def tile_picked_gatv_relu_p_kernel(
         seen = set()
         for z, c0, w in steps:
             codes, plane = weights[z]
-            picked = keep.tile([P, 2 * w], U8, name=f"picked{z}_{c0}", tag=f"picked{z}_{c0}", align_bytes=64)[:]
+            picked = keep.tile([P, 2 * w], U8, name=f"picked{z}_{c0}", tag="w_raw1" if (z, c0) == (0, 512) else f"picked{z}_{c0}", align_bytes=64)[:]
             nc.vector.tensor_copy(
                 picked.bitcast(U16),
                 word_tables[z][:].bitcast(U16).indirect(offs_sb[:, c0 // LIST_ROWS : (c0 + w) // LIST_ROWS]),
@@ -147,7 +152,7 @@ def tile_picked_gatv_relu_p_kernel(
                         lhsT=codes[:].bitcast(FP8X4),
                         lhsT_scale=plane[:],
                         rhs=picked[:, 2 * (g0 - c0) : 2 * (g0 - c0 + gw)].bitcast(FP4X4),
-                        rhs_scale=x_planes[:, z * S + g0 : z * S + g0 + gw],
+                        rhs_scale=x_planes[g0 // wide][:, z * wide + g0 % wide : z * wide + g0 % wide + gw],
                         start=not closing,
                         stop=closing,
                     )

@@ -51,33 +51,34 @@ def tile_picked_gatv_relu_p_kernel(
         nc.gpsimd.memset(score_rows[0:96], 0.0)
         nc.gpsimd.memset(score_rows[96:live], 0.0)
 
+        def load_list(d, pos):
+            tile = keep.tile([P, V // LIST_ROWS], U16, name=f"pos_sb{d}")
+            nc.sync.dma_start(tile[:], pos)
+            return tile
+
+        pos_sb = [load_list(0, pos1)]
         word_tables, w_raw = [], []
         for z in range(PASSES):
             rows = keep.tile([P, PACK, N], F32, name=f"w_raw{z}", tag=f"w_raw{z}", align_bytes=64)
             nc.sync.dma_start(rows[:], w1[z * P * PACK : (z + 1) * P * PACK, :].rearrange("(p j) m -> p j m", j=PACK))
             w_raw.append(rows)
-        for z in range(PASSES):
             table = keep.tile([P, 2 * T], U8, name=f"word_table{z}", tag=f"word_table{z}", align_bytes=64)
             nc.sync.dma_start(table[:].bitcast(I32), x_words[z].bitcast(I32))
             word_tables.append(table)
 
-        pos_sb = []
-        for d, pos in enumerate((pos1, pos2, pos3)):
-            tile = keep.tile([P, V // LIST_ROWS], U16, name=f"pos_sb{d}")
-            nc.sync.dma_start(tile[:], pos)
-            pos_sb.append(tile)
+        pos_sb.extend([load_list(1, pos2), load_list(2, pos3)])
 
-        wide = S // 2
-        x_planes = [keep.tile([P, PASSES * wide], U8, name=f"x_planes{h}", align_bytes=64) for h in range(2)]
+        parts = [(0, 768), (768, 256)]
+        x_planes = [keep.tile([P, PASSES * w], U8, name=f"x_planes{c0}", align_bytes=64) for c0, w in parts]
         for planes in x_planes:
             nc.vector.memset(planes[:].bitcast(I32), 0)
         ident = keep.tile([P, P], F32, name="ident")
         make_identity(nc, ident[:])
 
-        for h in range(2):
-            picked_scales = keep.tile([P, wide], U8, name=f"picked_scales{h}", align_bytes=64)
+        for h, (c0, w) in enumerate(parts):
+            picked_scales = keep.tile([P, w], U8, name=f"picked_scales{h}", align_bytes=64)
             nc.vector.tensor_copy(
-                picked_scales[:], scale_table[:].indirect(offs_sb[:, h * wide // LIST_ROWS : (h + 1) * wide // LIST_ROWS])
+                picked_scales[:], scale_table[:].indirect(offs_sb[:, c0 // LIST_ROWS : (c0 + w) // LIST_ROWS])
             )
             for q in range(4):
                 row = first + 8 * q
@@ -131,6 +132,11 @@ def tile_picked_gatv_relu_p_kernel(
             return [rows[:, i, :] for i in range(count)]
 
 
+        def x_plane(z, g0, gw):
+            h = 0 if g0 < parts[1][0] else 1
+            c0, w = parts[h]
+            return x_planes[h][:, z * w + g0 - c0 : z * w + g0 - c0 + gw]
+
         groups = [(0, 512), (512, 128), (640, 128), (768, 128), (896, 128)]
         banks = [psum.tile([P, w], F32, name=f"y_bank{g}", tag=f"bank{g}") for g, (c0, w) in enumerate(groups)]
         y = keep.tile([P, S], F32, name="y")
@@ -152,7 +158,7 @@ def tile_picked_gatv_relu_p_kernel(
                         lhsT=codes[:].bitcast(FP8X4),
                         lhsT_scale=plane[:],
                         rhs=picked[:, 2 * (g0 - c0) : 2 * (g0 - c0 + gw)].bitcast(FP4X4),
-                        rhs_scale=x_planes[g0 // wide][:, z * wide + g0 % wide : z * wide + g0 % wide + gw],
+                        rhs_scale=x_plane(z, g0, gw),
                         start=not closing,
                         stop=closing,
                     )
@@ -162,7 +168,7 @@ def tile_picked_gatv_relu_p_kernel(
                         nc.scalar.copy(y[:, g0 : g0 + gw], banks[g][:])
 
         inv = keep.tile([P, BLOCKS], F32, name="inv", tag="word_table1", align_bytes=64)
-        att = keep.tile([P, BLOCKS, D], F32, name="att", tag="picked1_512", align_bytes=64)
+        att = keep.tile([P, BLOCKS, D], F32, name="att", tag="picked1_768", align_bytes=64)
         nc.vector.reciprocal(inv[:], den[:])
         nc.vector.tensor_tensor(att[:], expd[:], inv[:].unsqueeze(2).to_broadcast([P, BLOCKS, D]), ALU.mult)
         att_rows = spread(0, 2, "bank1") + spread(2, 1, "bank2")

@@ -87,30 +87,34 @@ def tile_picked_gatv_relu_p_kernel(
                     picked_scales[row : row + 8, :].bitcast(I32),
                 )
 
-        def cast(z):
-            grouped = keep.tile([P, N, PACK], BF16, name=f"w_grouped{z}", tag=f"w_grouped{z}", align_bytes=64)
-            nc.scalar.copy(grouped[:], w_raw[z][:].rearrange("p j m -> p m j"))
-            return grouped
-
-        def quantise(z, grouped):
-            codes = keep.tile([P, N], U32, name=f"w_codes{z}", align_bytes=64)
-            plane = keep.tile([P, N], U8, name=f"w_plane{z}", align_bytes=64)
-            nc.vector.quantize_mx(
-                out=codes[:].bitcast(FP8X4), scales=plane[:], in_=grouped[:].rearrange("p m j -> p (m j)")
-            )
-            return codes, plane
-
-        weights = [quantise(z, cast(z)) for z in range(PASSES)]
+        grouped = keep.tile([P, PASSES * N, PACK], BF16, name="w_grouped", align_bytes=64)
+        for z in range(PASSES):
+            nc.scalar.copy(grouped[:, z * N : (z + 1) * N, :], w_raw[z][:].rearrange("p j m -> p m j"))
+        w_codes = keep.tile([P, PASSES * N], U32, name="w_codes", align_bytes=64)
+        w_planes = keep.tile([P, PASSES * N], U8, name="w_planes", align_bytes=64)
+        nc.vector.quantize_mx(
+            out=w_codes[:].bitcast(FP8X4), scales=w_planes[:], in_=grouped[:].rearrange("p m j -> p (m j)")
+        )
 
         score_bank = psum.tile([P, D, P], F32, name="score_bank", tag="bank7")
         for d in range(D):
             nc.tensor.transpose(score_bank[:, d, :], score_rows[:, d, :], ident[:])
-        low = keep.tile([P, BLOCKS], F32, name="low")
         expd = keep.tile([P, BLOCKS, D], F32, name="expd")
         den = keep.tile([P, BLOCKS], F32, name="den")
-        nc.vector.tensor_reduce(
-            low[:], score_bank[:, :, live:P].rearrange("p d b -> p b d"), AXIS.X, ALU.max, negate=True
-        )
+        low = keep.tile([P, BLOCKS], F32, name="low0")
+        nc.scalar.activation(low[:], score_bank[:, 0, live:P], ACT.Copy, scale=-1.0)
+        for d in range(1, D):
+            above = keep.tile([P, BLOCKS], F32, name=f"above{d}")
+            lower = keep.tile([P, BLOCKS], F32, name=f"low{d}")
+            for b in range(BLOCKS):
+                nc.scalar.activation(
+                    above[:, b : b + 1], score_bank[:, d, live + b : live + b + 1], ACT.Relu, bias=low[:, b : b + 1]
+                )
+            for b in range(BLOCKS):
+                nc.scalar.activation(
+                    lower[:, b : b + 1], above[:, b : b + 1], ACT.Identity, bias=low[:, b : b + 1], scale=-1.0
+                )
+            low = lower
         for b in range(BLOCKS):
             nc.scalar.activation(
                 expd[:, b, :], score_bank[:, :, live + b], ACT.Exp, bias=low[:, b : b + 1], accum_out=den[:, b : b + 1]
@@ -143,7 +147,6 @@ def tile_picked_gatv_relu_p_kernel(
         steps = [(0, 0, 512), (0, 512, 512), (1, 0, 512), (1, 512, 256), (1, 768, 256)]
         seen = set()
         for z, c0, w in steps:
-            codes, plane = weights[z]
             picked = keep.tile([P, 2 * w], U8, name=f"picked{z}_{c0}", tag="w_raw1" if (z, c0) == (0, 512) else f"picked{z}_{c0}", align_bytes=64)[:]
             nc.vector.tensor_copy(
                 picked.bitcast(U16),
@@ -155,8 +158,8 @@ def tile_picked_gatv_relu_p_kernel(
                     seen.add(g)
                     nc.tensor.matmul_mx(
                         out=banks[g][:],
-                        lhsT=codes[:].bitcast(FP8X4),
-                        lhsT_scale=plane[:],
+                        lhsT=w_codes[:, z * N : (z + 1) * N].bitcast(FP8X4),
+                        lhsT_scale=w_planes[:, z * N : (z + 1) * N],
                         rhs=picked[:, 2 * (g0 - c0) : 2 * (g0 - c0 + gw)].bitcast(FP4X4),
                         rhs_scale=x_plane(z, g0, gw),
                         start=not closing,
@@ -171,7 +174,7 @@ def tile_picked_gatv_relu_p_kernel(
         att = keep.tile([P, BLOCKS, D], F32, name="att", tag="picked1_768", align_bytes=64)
         nc.vector.reciprocal(inv[:], den[:])
         nc.vector.tensor_tensor(att[:], expd[:], inv[:].unsqueeze(2).to_broadcast([P, BLOCKS, D]), ALU.mult)
-        att_rows = spread(0, 2, "bank1") + spread(2, 1, "bank2")
+        att_rows = spread(0, 1, "bank1") + spread(1, 1, "bank2") + spread(2, 1, "bank0")
 
         sums = [psum.tile([P, P], F32, name=f"sum{b}", tag=f"bank{3 + b}") for b in range(turned_blocks)]
         for d in range(D):
@@ -187,7 +190,7 @@ def tile_picked_gatv_relu_p_kernel(
         low_result = keep.tile([P, half], F32, name="low_result")
         for b in range(turned_blocks):
             nc.scalar.activation(low_result[:, b * P : (b + 1) * P], sums[b][:], ACT.Relu)
-        nc.sync.dma_start(out[:, 0:half], low_result[:])
+        nc.scalar.dma_start(out[:, 0:half], low_result[:])
 
         def fetch(d, c0, w):
             term = keep.tile([P, w], F32, name=f"term{d}_{c0}")

@@ -174,7 +174,7 @@ def tile_picked_gatv_relu_p_kernel(
         att = keep.tile([P, BLOCKS, D], F32, name="att", tag="picked1_768", align_bytes=64)
         nc.vector.reciprocal(inv[:], den[:])
         nc.vector.tensor_tensor(att[:], expd[:], inv[:].unsqueeze(2).to_broadcast([P, BLOCKS, D]), ALU.mult)
-        att_rows = spread(0, 1, "bank1") + spread(1, 1, "bank2") + spread(2, 1, "bank0")
+        att_rows = spread(0, 1, "bank1") + spread(1, 2, "bank2")
 
         sums = [psum.tile([P, P], F32, name=f"sum{b}", tag=f"bank{3 + b}") for b in range(turned_blocks)]
         for d in range(D):
@@ -202,17 +202,17 @@ def tile_picked_gatv_relu_p_kernel(
             )
             return term
 
-        terms = [fetch(d, 0, half) for d in range(2)]
-        last = [fetch(2, 0, P)]
-        pair = keep.tile([P, half], F32, name="pair")
-        nc.vector.tensor_tensor(pair[:], terms[0][:], terms[1][:], ALU.add)
-        last.append(fetch(2, P, P))
-        totals = []
-        for i in range(2):
-            total = keep.tile([P, P], F32, name=f"total{i}")
-            nc.vector.tensor_tensor(total[:], pair[:, i * P : (i + 1) * P], last[i][:], ALU.add)
-            totals.append(total)
-        for i in range(2):
-            result = keep.tile([P, P], F32, name=f"result{i}")
-            nc.vector.tensor_scalar(result[:], totals[i][:], 0.0, None, ALU.max)
-            nc.sync.dma_start(out[:, half + i * P : half + (i + 1) * P], result[:])
+        terms = [fetch(d, 0, half) for d in range(D)]
+        pieces = [(0, 128), (128, 64), (192, 64)]
+        sums_so_far = [terms[0][:, c0 : c0 + w] for c0, w in pieces]
+        for d in range(1, D):
+            for i, (c0, w) in enumerate(pieces):
+                total = keep.tile([P, w], F32, name=f"total{d}_{c0}")
+                nc.vector.tensor_tensor(total[:], sums_so_far[i], terms[d][:, c0 : c0 + w], ALU.add)
+                sums_so_far[i] = total[:]
+        results = [keep.tile([P, P], F32, name=f"result{b}") for b in range(2)]
+        for i, (c0, w) in enumerate(pieces):
+            b = c0 // P
+            nc.vector.tensor_scalar(results[b][:, c0 % P : c0 % P + w], sums_so_far[i], 0.0, None, ALU.max)
+            if (c0 + w) % P == 0:
+                nc.sync.dma_start(out[:, half + b * P : half + (b + 1) * P], results[b][:])

@@ -165,6 +165,19 @@ def tile_picked_gatv_relu_p_kernel(
                         start=not closing,
                         stop=closing,
                     )
+                    if (z, g) == (0, 0):
+                        first_words = picked
+                    if (z, g) == (0, 2):
+                        spare = psum.tile([P, 512], F32, name="spare", tag="bank5")
+                        nc.tensor.matmul_mx(
+                            out=spare[:],
+                            lhsT=w_codes[:, 0:N].bitcast(FP8X4),
+                            lhsT_scale=w_planes[:, 0:N],
+                            rhs=first_words.bitcast(FP4X4),
+                            rhs_scale=x_plane(0, 0, 512),
+                            start=True,
+                            stop=True,
+                        )
                     if closing and g in (1, 2, 3):
                         nc.vector.tensor_copy(y[:, g0 : g0 + gw], banks[g][:])
                     elif closing:

@@ -193,17 +193,21 @@ def tile_picked_gatv_relu_p_kernel(
         for d in range(D):
             fetched = keep.tile([P, half], F32, name=f"fetched{d}")
             nc.vector.tensor_copy(fetched[:], y[:].indirect(pos_sb[d][:, 0 : half // LIST_ROWS]))
-            turned = psum.tile([P, turned_blocks, P], F32, name=f"turned{d}", tag=f"bank{5 + d}")
+            bank = psum.tile([P, turned_blocks, P], F32, name=f"turned{d}", tag=f"bank{5 + d}")
+            turned = [bank[:, b, :] for b in range(turned_blocks)]
+            if d == D - 1:
+                turned[0] = psum.tile([P, P], F32, name="turned_last", tag="bank0")[:]
             for b in range(turned_blocks):
-                nc.tensor.transpose(turned[:, b, :], fetched[:, b * P : (b + 1) * P], ident[:])
+                nc.tensor.transpose(turned[b], fetched[:, b * P : (b + 1) * P], ident[:])
             for b in range(turned_blocks):
                 weighted = keep.tile([P, P], F32, name=f"weighted{d}_{b}")
-                nc.scalar.activation(weighted[:], turned[:, b, :], ACT.Copy, scale=att[:, b, d : d + 1])
+                nc.scalar.activation(weighted[:], turned[b], ACT.Copy, scale=att[:, b, d : d + 1])
                 nc.tensor.matmul(sums[b][:], weighted[:], ident[:], start=(d == 0), stop=(d == D - 1), is_transpose=True)
-        low_result = keep.tile([P, half], F32, name="low_result")
+        clipped = [keep.tile([P, P], F32, name=f"clipped{b}") for b in range(turned_blocks)]
         for b in range(turned_blocks):
-            nc.scalar.activation(low_result[:, b * P : (b + 1) * P], sums[b][:], ACT.Relu)
-        nc.scalar.dma_start(out[:, 0:half], low_result[:])
+            nc.scalar.activation(clipped[b][:], sums[b][:], ACT.Relu)
+        for b in range(turned_blocks):
+            nc.scalar.dma_start(out[:, b * P : (b + 1) * P], clipped[b][:])
 
         def fetch(d, c0, w):
             term = keep.tile([P, w], F32, name=f"term{d}_{c0}")

@@ -200,14 +200,13 @@ def tile_picked_gatv_relu_p_kernel(
             for b in range(turned_blocks):
                 nc.tensor.transpose(turned[b], fetched[:, b * P : (b + 1) * P], ident[:])
             for b in range(turned_blocks):
-                weighted = keep.tile([P, P], F32, name=f"weighted{d}_{b}")
+                weighted = keep.tile([P, P], F32, name=f"weighted{d}_{b}", tag=f"weighted{d}_{b}")
                 nc.scalar.activation(weighted[:], turned[b], ACT.Copy, scale=att[:, b, d : d + 1])
                 nc.tensor.matmul(sums[b][:], weighted[:], ident[:], start=(d == 0), stop=(d == D - 1), is_transpose=True)
-        clipped = [keep.tile([P, P], F32, name=f"clipped{b}") for b in range(turned_blocks)]
+        clipped = keep.tile([P, half], F32, name="clipped")
         for b in range(turned_blocks):
-            nc.scalar.activation(clipped[b][:], sums[b][:], ACT.Relu)
-        for b in range(turned_blocks):
-            nc.scalar.dma_start(out[:, b * P : (b + 1) * P], clipped[b][:])
+            nc.scalar.activation(clipped[:, b * P : (b + 1) * P], sums[b][:], ACT.Relu)
+        nc.sync.dma_start(out[:, 0:half], clipped[:])
 
         def fetch(d, c0, w):
             term = keep.tile([P, w], F32, name=f"term{d}_{c0}")
@@ -223,10 +222,10 @@ def tile_picked_gatv_relu_p_kernel(
         pieces = [(0, 128), (128, 64), (192, 64)]
         sums_so_far = [terms[0][:, c0 : c0 + w] for c0, w in pieces]
         for d in range(1, D):
+            total = keep.tile([P, half], F32, name=f"total{d}", tag="weighted2_0" if d == 1 else "total")
             for i, (c0, w) in enumerate(pieces):
-                total = keep.tile([P, w], F32, name=f"total{d}_{c0}")
-                nc.vector.tensor_tensor(total[:], sums_so_far[i], terms[d][:, c0 : c0 + w], ALU.add)
-                sums_so_far[i] = total[:]
+                nc.vector.tensor_tensor(total[:, c0 : c0 + w], sums_so_far[i], terms[d][:, c0 : c0 + w], ALU.add)
+                sums_so_far[i] = total[:, c0 : c0 + w]
         results = [keep.tile([P, P], F32, name=f"result{b}") for b in range(2)]
         for i, (c0, w) in enumerate(pieces):
             b = c0 // P

@@ -45,28 +45,28 @@ def tile_picked_gatv_relu_p_kernel(
         )
         nc.vector.memset(scale_table[0:first, :].bitcast(I32), 0)
 
-        live = P - BLOCKS
-        score_rows = keep.tile([P, D, P], F32, name="score_rows", tag="score_rows", align_bytes=64)
-        nc.sync.dma_start(score_rows[live:P], score[:, 0, :].rearrange("d (b n) -> b d n", n=P))
-        nc.gpsimd.memset(score_rows[0:96], 0.0)
-        nc.gpsimd.memset(score_rows[96:live], 0.0)
-
         def load_list(d, pos):
             tile = keep.tile([P, V // LIST_ROWS], U16, name=f"pos_sb{d}")
             nc.sync.dma_start(tile[:], pos)
             return tile
 
-        pos_sb = [load_list(0, pos1)]
+        pos_sb = [load_list(0, pos1), load_list(1, pos2)]
         word_tables, w_raw = [], []
         for z in range(PASSES):
             rows = keep.tile([P, PACK, N], F32, name=f"w_raw{z}", tag=f"w_raw{z}", align_bytes=64)
             nc.sync.dma_start(rows[:], w1[z * P * PACK : (z + 1) * P * PACK, :].rearrange("(p j) m -> p j m", j=PACK))
             w_raw.append(rows)
+            if z == PASSES - 1:
+                live = P - BLOCKS
+                score_rows = keep.tile([P, D, P], F32, name="score_rows", tag="score_rows", align_bytes=64)
+                nc.sync.dma_start(score_rows[live:P], score[:, 0, :].rearrange("d (b n) -> b d n", n=P))
+                nc.gpsimd.memset(score_rows[0:96], 0.0)
+                nc.gpsimd.memset(score_rows[96:live], 0.0)
             table = keep.tile([P, 2 * T], U8, name=f"word_table{z}", tag=f"word_table{z}", align_bytes=64)
             nc.sync.dma_start(table[:].bitcast(I32), x_words[z].bitcast(I32))
             word_tables.append(table)
 
-        pos_sb.extend([load_list(1, pos2), load_list(2, pos3)])
+        pos_sb.append(load_list(2, pos3))
 
         parts = [(0, 768), (768, 256)]
         x_planes = [keep.tile([P, PASSES * w], U8, name=f"x_planes{c0}", align_bytes=64) for c0, w in parts]
@@ -187,7 +187,7 @@ def tile_picked_gatv_relu_p_kernel(
         att = keep.tile([P, BLOCKS, D], F32, name="att", tag="picked1_768", align_bytes=64)
         nc.vector.reciprocal(inv[:], den[:])
         nc.vector.tensor_tensor(att[:], expd[:], inv[:].unsqueeze(2).to_broadcast([P, BLOCKS, D]), ALU.mult)
-        att_rows = spread(0, 1, "bank1") + spread(1, 2, "bank2")
+        att_rows = spread(0, 1, "bank1") + spread(1, 1, "bank2") + spread(2, 1, "bank0")
 
         sums = [psum.tile([P, P], F32, name=f"sum{b}", tag=f"bank{3 + b}") for b in range(turned_blocks)]
         for d in range(D):
@@ -196,7 +196,7 @@ def tile_picked_gatv_relu_p_kernel(
             bank = psum.tile([P, turned_blocks, P], F32, name=f"turned{d}", tag=f"bank{5 + d}")
             turned = [bank[:, b, :] for b in range(turned_blocks)]
             if d == D - 1:
-                turned[0] = psum.tile([P, P], F32, name="turned_last", tag="bank0")[:]
+                turned[0] = psum.tile([P, P], F32, name="turned_last", tag="bank1")[:]
             for b in range(turned_blocks):
                 nc.tensor.transpose(turned[b], fetched[:, b * P : (b + 1) * P], ident[:])
             for b in range(turned_blocks):
@@ -222,7 +222,7 @@ def tile_picked_gatv_relu_p_kernel(
         pieces = [(0, 128), (128, 64), (192, 64)]
         sums_so_far = [terms[0][:, c0 : c0 + w] for c0, w in pieces]
         for d in range(1, D):
-            total = keep.tile([P, half], F32, name=f"total{d}", tag="weighted2_0" if d == 1 else "total")
+            total = keep.tile([P, half], F32, name=f"total{d}", tag="weighted1_1" if d == 1 else "total")
             for i, (c0, w) in enumerate(pieces):
                 nc.vector.tensor_tensor(total[:, c0 : c0 + w], sums_so_far[i], terms[d][:, c0 : c0 + w], ALU.add)
                 sums_so_far[i] = total[:, c0 : c0 + w]

@@ -35,7 +35,6 @@ def tile_picked_gatv_relu_p_kernel(
         psum = ctx.enter_context(tc.psum_pool(name="psum", bufs=1))
 
         offs_sb = keep.tile([P, S // LIST_ROWS], U16, name="offs_sb")
-        nc.sync.dma_start(offs_sb[:], offs)
 
         first = P - PASSES * SCALE_ROWS
         scale_table = keep.tile([P, T], U8, name="scale_table", align_bytes=64)
@@ -43,6 +42,7 @@ def tile_picked_gatv_relu_p_kernel(
             scale_table[first:P, :].bitcast(I32),
             x_scales.rearrange("z q c -> q z c").bitcast(I32),
         )
+        nc.sync.dma_start(offs_sb[:], offs)
         nc.vector.memset(scale_table[0:first, :].bitcast(I32), 0)
 
         def load_list(d, pos):
@@ -101,14 +101,22 @@ def tile_picked_gatv_relu_p_kernel(
             nc.tensor.transpose(score_bank[:, d, :], score_rows[:, d, :], ident[:])
         expd = keep.tile([P, BLOCKS, D], F32, name="expd")
         den = keep.tile([P, BLOCKS], F32, name="den")
+        floor_up = keep.tile([P, 1], F32, name="floor_up")
+        floor_down = keep.tile([P, 1], F32, name="floor_down")
+        nc.gpsimd.memset(floor_up[:], float(2**20))
+        nc.gpsimd.memset(floor_down[:], -float(2**20))
+        raised = keep.tile([P, D, BLOCKS], F32, name="raised")
+        floored = keep.tile([P, D, BLOCKS], F32, name="floored")
+        nc.scalar.activation(raised[:], score_bank[:, :, live:P], ACT.Relu, bias=floor_up[:])
+        nc.scalar.activation(floored[:], raised[:], ACT.Identity, bias=floor_down[:])
         low = keep.tile([P, BLOCKS], F32, name="low0")
-        nc.scalar.activation(low[:], score_bank[:, 0, live:P], ACT.Copy, scale=-1.0)
+        nc.scalar.activation(low[:], floored[:, 0, :], ACT.Copy, scale=-1.0)
         for d in range(1, D):
             above = keep.tile([P, BLOCKS], F32, name=f"above{d}")
             lower = keep.tile([P, BLOCKS], F32, name=f"low{d}")
             for b in range(BLOCKS):
                 nc.scalar.activation(
-                    above[:, b : b + 1], score_bank[:, d, live + b : live + b + 1], ACT.Relu, bias=low[:, b : b + 1]
+                    above[:, b : b + 1], floored[:, d, b : b + 1], ACT.Relu, bias=low[:, b : b + 1]
                 )
             for b in range(BLOCKS):
                 nc.scalar.activation(

@@ -50,7 +50,6 @@ def tile_picked_gatv_relu_p_kernel(
             nc.sync.dma_start(tile[:], pos)
             return tile
 
-        pos_sb = [load_list(0, pos1), load_list(1, pos2)]
         word_tables, w_raw = [], []
         for z in range(PASSES):
             rows = keep.tile([P, PACK, N], F32, name=f"w_raw{z}", tag=f"w_raw{z}", align_bytes=64)
@@ -66,7 +65,7 @@ def tile_picked_gatv_relu_p_kernel(
             nc.sync.dma_start(table[:].bitcast(I32), x_words[z].bitcast(I32))
             word_tables.append(table)
 
-        pos_sb.append(load_list(2, pos3))
+        pos_sb = [load_list(d, pos) for d, pos in enumerate((pos1, pos2, pos3))]
 
         parts = [(0, 768), (768, 256)]
         x_planes = [keep.tile([P, PASSES * w], U8, name=f"x_planes{c0}", align_bytes=64) for c0, w in parts]
@@ -89,7 +88,10 @@ def tile_picked_gatv_relu_p_kernel(
 
         grouped = keep.tile([P, PASSES * N, PACK], BF16, name="w_grouped", align_bytes=64)
         for z in range(PASSES):
-            nc.scalar.copy(grouped[:, z * N : (z + 1) * N, :], w_raw[z][:].rearrange("p j m -> p m j"))
+            nc.scalar.copy(
+                grouped[:, z * N : (z + 1) * N, :].rearrange("p (c i) j -> p c j i", i=PACK),
+                w_raw[z][:].rearrange("p j (c i) -> p c j i", i=PACK),
+            )
         w_codes = keep.tile([P, PASSES * N], U32, name="w_codes", align_bytes=64)
         w_planes = keep.tile([P, PASSES * N], U8, name="w_planes", align_bytes=64)
         nc.vector.quantize_mx(

@@ -34,6 +34,9 @@ def tile_picked_gatv_relu_p_kernel(
         keep = ctx.enter_context(tc.tile_pool(name="keep", bufs=1))
         psum = ctx.enter_context(tc.psum_pool(name="psum", bufs=1))
 
+        ident = keep.tile([P, P], F32, name="ident")
+        nc.vector.memset(ident[:], 0.0)
+        make_identity(nc, ident[:], nomemset=True)
         offs_sb = keep.tile([P, S // LIST_ROWS], U16, name="offs_sb")
 
         first = P - PASSES * SCALE_ROWS
@@ -59,8 +62,7 @@ def tile_picked_gatv_relu_p_kernel(
                 live = P - BLOCKS
                 score_rows = keep.tile([P, D, P], F32, name="score_rows", tag="score_rows", align_bytes=64)
                 nc.sync.dma_start(score_rows[live:P], score[:, 0, :].rearrange("d (b n) -> b d n", n=P))
-                nc.gpsimd.memset(score_rows[0:96], 0.0)
-                nc.gpsimd.memset(score_rows[96:live], 0.0)
+                nc.scalar.copy(score_rows[0:live], ident[0:live, :].unsqueeze(1).to_broadcast([live, D, P]))
             table = keep.tile([P, 2 * T], U8, name=f"word_table{z}", tag=f"word_table{z}", align_bytes=64)
             nc.sync.dma_start(table[:].bitcast(I32), x_words[z].bitcast(I32))
             word_tables.append(table)
@@ -71,8 +73,6 @@ def tile_picked_gatv_relu_p_kernel(
         x_planes = [keep.tile([P, PASSES * w], U8, name=f"x_planes{c0}", align_bytes=64) for c0, w in parts]
         for planes in x_planes:
             nc.vector.memset(planes[:].bitcast(I32), 0)
-        ident = keep.tile([P, P], F32, name="ident")
-        make_identity(nc, ident[:])
 
         for h, (c0, w) in enumerate(parts):
             picked_scales = keep.tile([P, w], U8, name=f"picked_scales{h}", align_bytes=64)
@@ -104,27 +104,23 @@ def tile_picked_gatv_relu_p_kernel(
         expd = keep.tile([P, BLOCKS, D], F32, name="expd")
         den = keep.tile([P, BLOCKS], F32, name="den")
         floor_up = keep.tile([P, 1], F32, name="floor_up")
-        floor_down = keep.tile([P, 1], F32, name="floor_down")
-        nc.gpsimd.memset(floor_up[:], float(2**20))
-        nc.gpsimd.memset(floor_down[:], -float(2**20))
+        nc.vector.memset(floor_up[:], float(2**20))
         raised = keep.tile([P, D, BLOCKS], F32, name="raised")
-        floored = keep.tile([P, D, BLOCKS], F32, name="floored")
         nc.scalar.activation(raised[:], score_bank[:, :, live:P], ACT.Relu, bias=floor_up[:])
-        nc.scalar.activation(floored[:], raised[:], ACT.Identity, bias=floor_down[:])
-        low = keep.tile([P, BLOCKS], F32, name="low0")
-        nc.scalar.activation(low[:], floored[:, 0, :], ACT.Copy, scale=-1.0)
-        for d in range(1, D):
-            above = keep.tile([P, BLOCKS], F32, name=f"above{d}")
-            lower = keep.tile([P, BLOCKS], F32, name=f"low{d}")
-            for b in range(BLOCKS):
-                nc.scalar.activation(
-                    above[:, b : b + 1], floored[:, d, b : b + 1], ACT.Relu, bias=low[:, b : b + 1]
-                )
-            for b in range(BLOCKS):
-                nc.scalar.activation(
-                    lower[:, b : b + 1], above[:, b : b + 1], ACT.Identity, bias=low[:, b : b + 1], scale=-1.0
-                )
-            low = lower
+        over01 = keep.tile([P, BLOCKS], F32, name="over01")
+        diff12 = keep.tile([P, BLOCKS], F32, name="diff12")
+        base = keep.tile([P, BLOCKS], F32, name="base")
+        over2 = keep.tile([P, BLOCKS], F32, name="over2")
+        low = keep.tile([P, BLOCKS], F32, name="low")
+        cols = [slice(b, b + 1) for b in range(BLOCKS)]
+        for c in cols:
+            nc.scalar.activation(over01[:, c], raised[:, 1, c], ACT.Relu, bias=raised[:, 0, c], scale=-1.0)
+            nc.scalar.activation(diff12[:, c], raised[:, 2, c], ACT.Identity, bias=raised[:, 1, c], scale=-1.0)
+        nc.scalar.activation(base[:], raised[:, 2, :], ACT.Identity, bias=floor_up[:], scale=-1.0)
+        for c in cols:
+            nc.scalar.activation(over2[:, c], over01[:, c], ACT.Relu, bias=diff12[:, c])
+        for c in cols:
+            nc.scalar.activation(low[:, c], over2[:, c], ACT.Identity, bias=base[:, c], scale=-1.0)
         for b in range(BLOCKS):
             nc.scalar.activation(
                 expd[:, b, :], score_bank[:, :, live + b], ACT.Exp, bias=low[:, b : b + 1], accum_out=den[:, b : b + 1]

@@ -62,7 +62,7 @@ def tile_picked_gatv_relu_p_kernel(
                 live = P - BLOCKS
                 score_rows = keep.tile([P, D, P], F32, name="score_rows", tag="score_rows", align_bytes=64)
                 nc.sync.dma_start(score_rows[live:P], score[:, 0, :].rearrange("d (b n) -> b d n", n=P))
-                nc.scalar.copy(score_rows[0:live], ident[0:live, :].unsqueeze(1).to_broadcast([live, D, P]))
+                nc.vector.memset(score_rows[0:live], 0.0)
             table = keep.tile([P, 2 * T], U8, name=f"word_table{z}", tag=f"word_table{z}", align_bytes=64)
             nc.sync.dma_start(table[:].bitcast(I32), x_words[z].bitcast(I32))
             word_tables.append(table)

@@ -48,6 +48,11 @@ def tile_picked_gatv_relu_p_kernel(
         nc.sync.dma_start(offs_sb[:], offs)
         nc.vector.memset(scale_table[0:first, :].bitcast(I32), 0)
 
+        live = P - BLOCKS
+        score_rows = keep.tile([P, D, P], F32, name="score_rows", tag="score_rows", align_bytes=64)
+        nc.sync.dma_start(score_rows[live:P], score[:, 0, :].rearrange("d (b n) -> b d n", n=P))
+        nc.vector.memset(score_rows[0:live], 0.0)
+
         def load_list(d, pos):
             tile = keep.tile([P, V // LIST_ROWS], U16, name=f"pos_sb{d}")
             nc.sync.dma_start(tile[:], pos)
@@ -58,11 +63,6 @@ def tile_picked_gatv_relu_p_kernel(
             rows = keep.tile([P, PACK, N], F32, name=f"w_raw{z}", tag=f"w_raw{z}", align_bytes=64)
             nc.sync.dma_start(rows[:], w1[z * P * PACK : (z + 1) * P * PACK, :].rearrange("(p j) m -> p j m", j=PACK))
             w_raw.append(rows)
-            if z == PASSES - 1:
-                live = P - BLOCKS
-                score_rows = keep.tile([P, D, P], F32, name="score_rows", tag="score_rows", align_bytes=64)
-                nc.sync.dma_start(score_rows[live:P], score[:, 0, :].rearrange("d (b n) -> b d n", n=P))
-                nc.vector.memset(score_rows[0:live], 0.0)
             table = keep.tile([P, 2 * T], U8, name=f"word_table{z}", tag=f"word_table{z}", align_bytes=64)
             nc.sync.dma_start(table[:].bitcast(I32), x_words[z].bitcast(I32))
             word_tables.append(table)
@@ -107,40 +107,45 @@ def tile_picked_gatv_relu_p_kernel(
         nc.vector.memset(floor_up[:], float(2**20))
         raised = keep.tile([P, D, BLOCKS], F32, name="raised")
         nc.scalar.activation(raised[:], score_bank[:, :, live:P], ACT.Relu, bias=floor_up[:])
+        base = keep.tile([P, BLOCKS], F32, name="base")
+        nc.scalar.activation(base[:], raised[:, 2, :], ACT.Identity, bias=floor_up[:], scale=-1.0)
         over01 = keep.tile([P, BLOCKS], F32, name="over01")
         diff12 = keep.tile([P, BLOCKS], F32, name="diff12")
-        base = keep.tile([P, BLOCKS], F32, name="base")
         over2 = keep.tile([P, BLOCKS], F32, name="over2")
         low = keep.tile([P, BLOCKS], F32, name="low")
-        cols = [slice(b, b + 1) for b in range(BLOCKS)]
-        for c in cols:
-            nc.scalar.activation(over01[:, c], raised[:, 1, c], ACT.Relu, bias=raised[:, 0, c], scale=-1.0)
-            nc.scalar.activation(diff12[:, c], raised[:, 2, c], ACT.Identity, bias=raised[:, 1, c], scale=-1.0)
-        nc.scalar.activation(base[:], raised[:, 2, :], ACT.Identity, bias=floor_up[:], scale=-1.0)
-        for c in cols:
-            nc.scalar.activation(over2[:, c], over01[:, c], ACT.Relu, bias=diff12[:, c])
-        for c in cols:
-            nc.scalar.activation(low[:, c], over2[:, c], ACT.Identity, bias=base[:, c], scale=-1.0)
-        for b in range(BLOCKS):
-            nc.scalar.activation(
-                expd[:, b, :], score_bank[:, :, live + b], ACT.Exp, bias=low[:, b : b + 1], accum_out=den[:, b : b + 1]
-            )
+
+        def exponentials(blocks):
+            cols = [slice(b, b + 1) for b in blocks]
+            for c in cols:
+                nc.scalar.activation(over01[:, c], raised[:, 1, c], ACT.Relu, bias=raised[:, 0, c], scale=-1.0)
+                nc.scalar.activation(diff12[:, c], raised[:, 2, c], ACT.Identity, bias=raised[:, 1, c], scale=-1.0)
+            for c in cols:
+                nc.scalar.activation(over2[:, c], over01[:, c], ACT.Relu, bias=diff12[:, c])
+            for c in cols:
+                nc.scalar.activation(low[:, c], over2[:, c], ACT.Identity, bias=base[:, c], scale=-1.0)
+            for b in blocks:
+                nc.scalar.activation(
+                    expd[:, b, :], score_bank[:, :, live + b], ACT.Exp, bias=low[:, b : b + 1], accum_out=den[:, b : b + 1]
+                )
 
         half = V // 2
         turned_blocks = half // P
 
-        def spread(first_d, count, tag):
-            bank = psum.tile([P, count, half], F32, name=f"att_bank{first_d}", tag=tag)
-            for i in range(count):
-                for b in range(turned_blocks, BLOCKS):
-                    c0 = (b - turned_blocks) * P
-                    nc.tensor.transpose(
-                        bank[:, i, c0 : c0 + P], att[:, b, first_d + i : first_d + i + 1].to_broadcast([P, P]), ident[:]
-                    )
-            rows = keep.tile([P, count, half], F32, name=f"att_rows{first_d}")
-            nc.scalar.copy(rows[:], bank[:])
-            return [rows[:, i, :] for i in range(count)]
+        def spread(bank, column):
+            for b in range(turned_blocks, BLOCKS):
+                c0 = (b - turned_blocks) * P
+                nc.tensor.transpose(bank[:, c0 : c0 + P], column(b).to_broadcast([P, P]), ident[:])
 
+        exponentials(range(turned_blocks, BLOCKS))
+        exp_rows = []
+        for first_d, count, tag in ((0, 2, "bank5"), (2, 1, "bank6")):
+            bank = psum.tile([P, count, half], F32, name=f"exp_bank{first_d}", tag=tag)
+            for i in range(count):
+                spread(bank[:, i, :], lambda b: expd[:, b, first_d + i : first_d + i + 1])
+            rows = keep.tile([P, count, half], F32, name=f"exp_rows{first_d}")
+            nc.scalar.copy(rows[:], bank[:])
+            exp_rows.extend(rows[:, i, :] for i in range(count))
+        exponentials(range(turned_blocks))
 
         def x_plane(z, g0, gw):
             h = 0 if g0 < parts[1][0] else 1
@@ -174,7 +179,7 @@ def tile_picked_gatv_relu_p_kernel(
                     if (z, g) == (0, 0):
                         first_words = picked
                     if (z, g) == (0, 2):
-                        spare = psum.tile([P, 512], F32, name="spare", tag="bank5")
+                        spare = psum.tile([P, 512], F32, name="spare", tag="bank7")
                         nc.tensor.matmul_mx(
                             out=spare[:],
                             lhsT=w_codes[:, 0:N].bitcast(FP8X4),
@@ -190,51 +195,60 @@ def tile_picked_gatv_relu_p_kernel(
                         nc.scalar.copy(y[:, g0 : g0 + gw], banks[g][:])
 
         inv = keep.tile([P, BLOCKS], F32, name="inv", tag="word_table1", align_bytes=64)
-        att = keep.tile([P, BLOCKS, D], F32, name="att", tag="picked1_768", align_bytes=64)
+        att = keep.tile([P, turned_blocks, D], F32, name="att", tag="picked1_768", align_bytes=64)
         nc.vector.reciprocal(inv[:], den[:])
-        nc.vector.tensor_tensor(att[:], expd[:], inv[:].unsqueeze(2).to_broadcast([P, BLOCKS, D]), ALU.mult)
-        att_rows = spread(0, 1, "bank1") + spread(1, 1, "bank2") + spread(2, 1, "bank0")
+        nc.vector.tensor_tensor(
+            att[:], expd[:, 0:turned_blocks, :], inv[:, 0:turned_blocks].unsqueeze(2).to_broadcast([P, turned_blocks, D]), ALU.mult
+        )
+        inv_rows = psum.tile([P, half], F32, name="inv_rows", tag="bank4")
+        spread(inv_rows[:], lambda b: inv[:, b : b + 1])
 
-        sums = [psum.tile([P, P], F32, name=f"sum{b}", tag=f"bank{3 + b}") for b in range(turned_blocks)]
+        sums = [psum.tile([P, P], F32, name=f"sum{b}", tag=f"bank{2 + b}") for b in range(turned_blocks)]
+        turned = []
         for d in range(D):
             fetched = keep.tile([P, half], F32, name=f"fetched{d}")
-            nc.vector.tensor_copy(fetched[:], y[:].indirect(pos_sb[d][:, 0 : half // LIST_ROWS]))
-            bank = psum.tile([P, turned_blocks, P], F32, name=f"turned{d}", tag=f"bank{5 + d}")
-            turned = [bank[:, b, :] for b in range(turned_blocks)]
-            if d == D - 1:
-                turned[0] = psum.tile([P, P], F32, name="turned_last", tag="bank1")[:]
+            on_scalar = half if d < D - 1 else P
+            nc.scalar.activation(fetched[:, 0:on_scalar], y[:].indirect(pos_sb[d][:, 0 : on_scalar // LIST_ROWS]), ACT.Copy)
+            if on_scalar < half:
+                nc.vector.tensor_copy(
+                    fetched[:, on_scalar:half], y[:].indirect(pos_sb[d][:, on_scalar // LIST_ROWS : half // LIST_ROWS])
+                )
+            if d < D - 1:
+                bank = psum.tile([P, turned_blocks, P], F32, name=f"turned{d}", tag=f"bank{d}")
+                turned.append([bank[:, b, :] for b in range(turned_blocks)])
+            else:
+                turned.append([psum.tile([P, P], F32, name=f"turned{d}_{b}", tag=f"bank{5 + b}")[:] for b in range(turned_blocks)])
             for b in range(turned_blocks):
-                nc.tensor.transpose(turned[b], fetched[:, b * P : (b + 1) * P], ident[:])
-            for b in range(turned_blocks):
+                nc.tensor.transpose(turned[d][b], fetched[:, b * P : (b + 1) * P], ident[:])
+        for d in range(D):
+            for b in reversed(range(turned_blocks)):
                 weighted = keep.tile([P, P], F32, name=f"weighted{d}_{b}", tag=f"weighted{d}_{b}")
-                nc.scalar.activation(weighted[:], turned[b], ACT.Copy, scale=att[:, b, d : d + 1])
+                nc.scalar.activation(weighted[:], turned[d][b], ACT.Copy, scale=att[:, b, d : d + 1])
                 nc.tensor.matmul(sums[b][:], weighted[:], ident[:], start=(d == 0), stop=(d == D - 1), is_transpose=True)
-        clipped = keep.tile([P, half], F32, name="clipped")
-        for b in range(turned_blocks):
-            nc.scalar.activation(clipped[:, b * P : (b + 1) * P], sums[b][:], ACT.Relu)
-        nc.sync.dma_start(out[:, 0:half], clipped[:])
 
-        def fetch(d, c0, w):
-            term = keep.tile([P, w], F32, name=f"term{d}_{c0}")
+        def fetch(d):
+            term = keep.tile([P, half], F32, name=f"term{d}")
             nc.vector.tensor_tensor(
-                term[:],
-                y[:].indirect(pos_sb[d][:, (half + c0) // LIST_ROWS : (half + c0 + w) // LIST_ROWS]),
-                att_rows[d][:, c0 : c0 + w],
-                ALU.mult,
+                term[:], y[:].indirect(pos_sb[d][:, half // LIST_ROWS : V // LIST_ROWS]), exp_rows[d], ALU.mult
             )
             return term
 
-        terms = [fetch(d, 0, half) for d in range(D)]
+        terms = [fetch(d) for d in range(D)]
         pieces = [(0, 128), (128, 64), (192, 64)]
         sums_so_far = [terms[0][:, c0 : c0 + w] for c0, w in pieces]
         for d in range(1, D):
-            total = keep.tile([P, half], F32, name=f"total{d}", tag="weighted1_1" if d == 1 else "total")
+            total = keep.tile([P, half], F32, name=f"total{d}")
             for i, (c0, w) in enumerate(pieces):
                 nc.vector.tensor_tensor(total[:, c0 : c0 + w], sums_so_far[i], terms[d][:, c0 : c0 + w], ALU.add)
                 sums_so_far[i] = total[:, c0 : c0 + w]
-        results = [keep.tile([P, P], F32, name=f"result{b}") for b in range(2)]
+        result = keep.tile([P, half], F32, name="result")
         for i, (c0, w) in enumerate(pieces):
-            b = c0 // P
-            nc.vector.tensor_scalar(results[b][:, c0 % P : c0 % P + w], sums_so_far[i], 0.0, None, ALU.max)
-            if (c0 + w) % P == 0:
-                nc.sync.dma_start(out[:, half + b * P : half + (b + 1) * P], results[b][:])
+            nc.vector.scalar_tensor_tensor(
+                result[:, c0 : c0 + w], sums_so_far[i], 0.0, inv_rows[:, c0 : c0 + w], ALU.max, ALU.mult
+            )
+        nc.sync.dma_start(out[:, half:V], result[:])
+
+        clipped = keep.tile([P, half], F32, name="clipped")
+        for b in reversed(range(turned_blocks)):
+            nc.scalar.activation(clipped[:, b * P : (b + 1) * P], sums[b][:], ACT.Relu)
+        nc.sync.dma_start(out[:, 0:half], clipped[:])

@@ -33,7 +33,10 @@ def tile_picked_gatv_relu_p_kernel(
     with ExitStack() as ctx:
         keep = ctx.enter_context(tc.tile_pool(name="keep", bufs=1))
         psum = ctx.enter_context(tc.psum_pool(name="psum", bufs=1))
+        reused = ctx.enter_context(tc.tile_pool(name="reused", bufs=1))
 
+        floor_up = keep.tile([P, 1], F32, name="floor_up")
+        nc.vector.memset(floor_up[:], float(2**20))
         ident = keep.tile([P, P], F32, name="ident")
         nc.vector.memset(ident[:], 0.0)
         make_identity(nc, ident[:], nomemset=True)
@@ -58,14 +61,23 @@ def tile_picked_gatv_relu_p_kernel(
             nc.sync.dma_start(tile[:], pos)
             return tile
 
-        word_tables, w_raw = [], []
-        for z in range(PASSES):
-            rows = keep.tile([P, PACK, N], F32, name=f"w_raw{z}", tag=f"w_raw{z}", align_bytes=64)
-            nc.sync.dma_start(rows[:], w1[z * P * PACK : (z + 1) * P * PACK, :].rearrange("(p j) m -> p j m", j=PACK))
-            w_raw.append(rows)
+        def load_words(z):
             table = keep.tile([P, 2 * T], U8, name=f"word_table{z}", tag=f"word_table{z}", align_bytes=64)
             nc.sync.dma_start(table[:].bitcast(I32), x_words[z].bitcast(I32))
-            word_tables.append(table)
+            return table
+
+        def load_weights(z):
+            if z == 0:
+                rows = keep.tile([P, PACK, N], F32, name="w_raw0", tag="w_raw0", align_bytes=64)
+            else:
+                rows = reused.tile([P, PACK, N], F32, name="w_raw1", offset=0, align_bytes=64)
+            nc.sync.dma_start(rows[:], w1[z * P * PACK : (z + 1) * P * PACK, :].rearrange("(p j) m -> p j m", j=PACK))
+            return rows
+
+        w_raw, word_tables = [], []
+        for z in range(PASSES):
+            w_raw.append(load_weights(z))
+            word_tables.append(load_words(z))
 
         pos_sb = [load_list(d, pos) for d, pos in enumerate((pos1, pos2, pos3))]
 
@@ -86,47 +98,42 @@ def tile_picked_gatv_relu_p_kernel(
                     picked_scales[row : row + 8, :].bitcast(I32),
                 )
 
-        grouped = keep.tile([P, PASSES * N, PACK], BF16, name="w_grouped", align_bytes=64)
-        for z in range(PASSES):
-            nc.scalar.copy(
-                grouped[:, z * N : (z + 1) * N, :].rearrange("p (c i) j -> p c j i", i=PACK),
-                w_raw[z][:].rearrange("p j (c i) -> p c j i", i=PACK),
-            )
-        w_codes = keep.tile([P, PASSES * N], U32, name="w_codes", align_bytes=64)
-        w_planes = keep.tile([P, PASSES * N], U8, name="w_planes", align_bytes=64)
-        nc.vector.quantize_mx(
-            out=w_codes[:].bitcast(FP8X4), scales=w_planes[:], in_=grouped[:].rearrange("p m j -> p (m j)")
-        )
-
         score_bank = psum.tile([P, D, P], F32, name="score_bank", tag="bank7")
         for d in range(D):
             nc.tensor.transpose(score_bank[:, d, :], score_rows[:, d, :], ident[:])
-        expd = keep.tile([P, BLOCKS, D], F32, name="expd")
         den = keep.tile([P, BLOCKS], F32, name="den")
-        floor_up = keep.tile([P, 1], F32, name="floor_up")
-        nc.vector.memset(floor_up[:], float(2**20))
-        raised = keep.tile([P, D, BLOCKS], F32, name="raised")
-        nc.scalar.activation(raised[:], score_bank[:, :, live:P], ACT.Relu, bias=floor_up[:])
-        base = keep.tile([P, BLOCKS], F32, name="base")
-        nc.scalar.activation(base[:], raised[:, 2, :], ACT.Identity, bias=floor_up[:], scale=-1.0)
-        over01 = keep.tile([P, BLOCKS], F32, name="over01")
-        diff12 = keep.tile([P, BLOCKS], F32, name="diff12")
-        over2 = keep.tile([P, BLOCKS], F32, name="over2")
-        low = keep.tile([P, BLOCKS], F32, name="low")
 
-        def exponentials(blocks):
-            cols = [slice(b, b + 1) for b in blocks]
+        def exponentials(first_block, count, tags):
+            scores = score_bank[:, :, live + first_block : live + first_block + count]
+            raised = keep.tile([P, D, count], F32, name=f"raised{first_block}", tag=tags["raised"])
+            nc.scalar.activation(raised[:], scores, ACT.Relu, bias=floor_up[:])
+            base, over01, diff12, over2 = (
+                keep.tile([P, count], F32, name=f"{name}{first_block}", tag=tags.get(name, f"{name}{first_block}"), align_bytes=64)
+                for name in ("base", "over01", "diff12", "over2")
+            )
+            if first_block:
+                low = keep.tile([P, count], F32, name="low_direct", tag="w_grouped1", align_bytes=64)
+            else:
+                low = keep.tile([P, count], F32, name="low0", tag="low0", align_bytes=64)
+            expd = keep.tile([P, count, D], F32, name=f"expd{first_block}", tag=tags["expd"])
+            cols = [slice(b, b + 1) for b in range(count)]
             for c in cols:
                 nc.scalar.activation(over01[:, c], raised[:, 1, c], ACT.Relu, bias=raised[:, 0, c], scale=-1.0)
                 nc.scalar.activation(diff12[:, c], raised[:, 2, c], ACT.Identity, bias=raised[:, 1, c], scale=-1.0)
+            nc.scalar.activation(base[:], raised[:, 2, :], ACT.Identity, bias=floor_up[:], scale=-1.0)
             for c in cols:
                 nc.scalar.activation(over2[:, c], over01[:, c], ACT.Relu, bias=diff12[:, c])
             for c in cols:
                 nc.scalar.activation(low[:, c], over2[:, c], ACT.Identity, bias=base[:, c], scale=-1.0)
-            for b in blocks:
+            for b in range(count):
                 nc.scalar.activation(
-                    expd[:, b, :], score_bank[:, :, live + b], ACT.Exp, bias=low[:, b : b + 1], accum_out=den[:, b : b + 1]
+                    expd[:, b, :],
+                    scores[:, :, b],
+                    ACT.Exp,
+                    bias=low[:, b : b + 1],
+                    accum_out=den[:, first_block + b : first_block + b + 1],
                 )
+            return expd
 
         half = V // 2
         turned_blocks = half // P
@@ -136,16 +143,29 @@ def tile_picked_gatv_relu_p_kernel(
                 c0 = (b - turned_blocks) * P
                 nc.tensor.transpose(bank[:, c0 : c0 + P], column(b).to_broadcast([P, P]), ident[:])
 
-        exponentials(range(turned_blocks, BLOCKS))
+        expd_direct = exponentials(turned_blocks, BLOCKS - turned_blocks, {"raised": "raised_direct", "expd": "expd_direct"})
+        w_codes, w_planes = [], []
+        for z in range(PASSES):
+            grouped = keep.tile([P, N, PACK], BF16, name=f"w_grouped{z}", tag=f"w_grouped{z}", align_bytes=64)
+            nc.scalar.copy(
+                grouped[:].rearrange("p (c i) j -> p c j i", i=PACK),
+                w_raw[z][:].rearrange("p j (c i) -> p c j i", i=PACK),
+            )
+            w_codes.append(keep.tile([P, N], U32, name=f"w_codes{z}", align_bytes=64))
+            w_planes.append(keep.tile([P, N], U8, name=f"w_planes{z}", align_bytes=64))
+            nc.vector.quantize_mx(
+                out=w_codes[z][:].bitcast(FP8X4), scales=w_planes[z][:], in_=grouped[:].rearrange("p m j -> p (m j)")
+            )
+
         exp_rows = []
         for first_d, count, tag in ((0, 2, "bank5"), (2, 1, "bank6")):
             bank = psum.tile([P, count, half], F32, name=f"exp_bank{first_d}", tag=tag)
             for i in range(count):
-                spread(bank[:, i, :], lambda b: expd[:, b, first_d + i : first_d + i + 1])
+                spread(bank[:, i, :], lambda b: expd_direct[:, b - turned_blocks, first_d + i : first_d + i + 1])
             rows = keep.tile([P, count, half], F32, name=f"exp_rows{first_d}")
             nc.scalar.copy(rows[:], bank[:])
             exp_rows.extend(rows[:, i, :] for i in range(count))
-        exponentials(range(turned_blocks))
+        expd_turned = exponentials(0, turned_blocks, {"raised": "expd_direct", "expd": "expd_turned"})
 
         def x_plane(z, g0, gw):
             h = 0 if g0 < parts[1][0] else 1
@@ -153,12 +173,23 @@ def tile_picked_gatv_relu_p_kernel(
             return x_planes[h][:, z * w + g0 - c0 : z * w + g0 - c0 + gw]
 
         groups = [(0, 512), (512, 128), (640, 128), (768, 128), (896, 128)]
+        spare = psum.tile([P, 512], F32, name="spare", tag="bank3")
         banks = [psum.tile([P, w], F32, name=f"y_bank{g}", tag=f"bank{g}") for g, (c0, w) in enumerate(groups)]
-        y = keep.tile([P, S], F32, name="y")
+        y = keep.tile([P, S], F32, name="y", tag="low0", align_bytes=64)
         steps = [(0, 0, 512), (0, 512, 512), (1, 0, 512), (1, 512, 256), (1, 768, 256)]
+        picked_tiles = {
+            (1, c0): reused.tile([P, 2 * w], U8, name=f"picked1_{c0}", offset=2 * c0, align_bytes=64)[:]
+            for z, c0, w in steps
+            if z == 1
+        }
+        picked_tiles[0, 0] = keep.tile([P, S], U8, name="picked0_0", align_bytes=64)[:]
+        picked_tiles[0, 512] = keep.tile([P, S], U8, name="picked0_512", tag="w_raw0", align_bytes=64)[:]
+        inv = keep.tile([P, BLOCKS], F32, name="inv")
+        att = keep.tile([P, turned_blocks, D], F32, name="att")
+        nc.vector.reciprocal(inv[:], den[:])
         seen = set()
         for z, c0, w in steps:
-            picked = keep.tile([P, 2 * w], U8, name=f"picked{z}_{c0}", tag="w_raw1" if (z, c0) == (0, 512) else f"picked{z}_{c0}", align_bytes=64)[:]
+            picked = picked_tiles[z, c0]
             nc.vector.tensor_copy(
                 picked.bitcast(U16),
                 word_tables[z][:].bitcast(U16).indirect(offs_sb[:, c0 // LIST_ROWS : (c0 + w) // LIST_ROWS]),
@@ -169,8 +200,8 @@ def tile_picked_gatv_relu_p_kernel(
                     seen.add(g)
                     nc.tensor.matmul_mx(
                         out=banks[g][:],
-                        lhsT=w_codes[:, z * N : (z + 1) * N].bitcast(FP8X4),
-                        lhsT_scale=w_planes[:, z * N : (z + 1) * N],
+                        lhsT=w_codes[z][:].bitcast(FP8X4),
+                        lhsT_scale=w_planes[z][:],
                         rhs=picked[:, 2 * (g0 - c0) : 2 * (g0 - c0 + gw)].bitcast(FP4X4),
                         rhs_scale=x_plane(z, g0, gw),
                         start=not closing,
@@ -179,27 +210,27 @@ def tile_picked_gatv_relu_p_kernel(
                     if (z, g) == (0, 0):
                         first_words = picked
                     if (z, g) == (0, 2):
-                        spare = psum.tile([P, 512], F32, name="spare", tag="bank7")
                         nc.tensor.matmul_mx(
                             out=spare[:],
-                            lhsT=w_codes[:, 0:N].bitcast(FP8X4),
-                            lhsT_scale=w_planes[:, 0:N],
+                            lhsT=w_codes[0][:].bitcast(FP8X4),
+                            lhsT_scale=w_planes[0][:],
                             rhs=first_words.bitcast(FP4X4),
                             rhs_scale=x_plane(0, 0, 512),
                             start=True,
                             stop=True,
+                        )
+                    if closing and g == 3:
+                        nc.vector.tensor_tensor(
+                            att[:],
+                            expd_turned[:],
+                            inv[:, 0:turned_blocks].unsqueeze(2).to_broadcast([P, turned_blocks, D]),
+                            ALU.mult,
                         )
                     if closing and g in (1, 2, 3):
                         nc.vector.tensor_copy(y[:, g0 : g0 + gw], banks[g][:])
                     elif closing:
                         nc.scalar.copy(y[:, g0 : g0 + gw], banks[g][:])
 
-        inv = keep.tile([P, BLOCKS], F32, name="inv", tag="word_table1", align_bytes=64)
-        att = keep.tile([P, turned_blocks, D], F32, name="att", tag="picked1_768", align_bytes=64)
-        nc.vector.reciprocal(inv[:], den[:])
-        nc.vector.tensor_tensor(
-            att[:], expd[:, 0:turned_blocks, :], inv[:, 0:turned_blocks].unsqueeze(2).to_broadcast([P, turned_blocks, D]), ALU.mult
-        )
         inv_rows = psum.tile([P, half], F32, name="inv_rows", tag="bank4")
         spread(inv_rows[:], lambda b: inv[:, b : b + 1])
 

@@ -34,9 +34,8 @@ def tile_picked_gatv_relu_p_kernel(
         keep = ctx.enter_context(tc.tile_pool(name="keep", bufs=1))
         psum = ctx.enter_context(tc.psum_pool(name="psum", bufs=1))
         reused = ctx.enter_context(tc.tile_pool(name="reused", bufs=1))
+        early = ctx.enter_context(tc.tile_pool(name="early", bufs=1))
 
-        floor_up = keep.tile([P, 1], F32, name="floor_up")
-        nc.vector.memset(floor_up[:], float(2**20))
         ident = keep.tile([P, P], F32, name="ident")
         nc.vector.memset(ident[:], 0.0)
         make_identity(nc, ident[:], nomemset=True)
@@ -52,7 +51,7 @@ def tile_picked_gatv_relu_p_kernel(
         nc.vector.memset(scale_table[0:first, :].bitcast(I32), 0)
 
         live = P - BLOCKS
-        score_rows = keep.tile([P, D, P], F32, name="score_rows", tag="score_rows", align_bytes=64)
+        score_rows = early.tile([P, D, P], F32, name="score_rows", offset=256, align_bytes=64)
         nc.sync.dma_start(score_rows[live:P], score[:, 0, :].rearrange("d (b n) -> b d n", n=P))
         nc.vector.memset(score_rows[0:live], 0.0)
 
@@ -68,7 +67,7 @@ def tile_picked_gatv_relu_p_kernel(
 
         def load_weights(z):
             if z == 0:
-                rows = keep.tile([P, PACK, N], F32, name="w_raw0", tag="w_raw0", align_bytes=64)
+                rows = early.tile([P, PACK, N], F32, name="w_raw0", offset=1792, align_bytes=64)
             else:
                 rows = reused.tile([P, PACK, N], F32, name="w_raw1", offset=0, align_bytes=64)
             nc.sync.dma_start(rows[:], w1[z * P * PACK : (z + 1) * P * PACK, :].rearrange("(p j) m -> p j m", j=PACK))
@@ -86,8 +85,18 @@ def tile_picked_gatv_relu_p_kernel(
         for planes in x_planes:
             nc.vector.memset(planes[:].bitcast(I32), 0)
 
+        score_bank = psum.tile([P, D, P], F32, name="score_bank", tag="bank7")
+        for d in range(D):
+            nc.tensor.transpose(score_bank[:, d, :], score_rows[:, d, :], ident[:])
+        scores = score_bank[:, :, live:P]
+        low = keep.tile([P, BLOCKS], F32, name="low", tag="w_grouped1", align_bytes=64)
+
         for h, (c0, w) in enumerate(parts):
-            picked_scales = keep.tile([P, w], U8, name=f"picked_scales{h}", align_bytes=64)
+            if h == 1:
+                nc.vector.tensor_reduce(low[:], scores.rearrange("p d b -> p b d"), AXIS.X, ALU.max, negate=True)
+                picked_scales = early.tile([P, w], U8, name="picked_scales1", offset=64, align_bytes=64)
+            else:
+                picked_scales = keep.tile([P, w], U8, name="picked_scales0", align_bytes=64)
             nc.vector.tensor_copy(
                 picked_scales[:], scale_table[:].indirect(offs_sb[:, c0 // LIST_ROWS : (c0 + w) // LIST_ROWS])
             )
@@ -98,52 +107,17 @@ def tile_picked_gatv_relu_p_kernel(
                     picked_scales[row : row + 8, :].bitcast(I32),
                 )
 
-        score_bank = psum.tile([P, D, P], F32, name="score_bank", tag="bank7")
-        for d in range(D):
-            nc.tensor.transpose(score_bank[:, d, :], score_rows[:, d, :], ident[:])
         den = keep.tile([P, BLOCKS], F32, name="den")
-
-        def exponentials(first_block, count, tags):
-            scores = score_bank[:, :, live + first_block : live + first_block + count]
-            raised = keep.tile([P, D, count], F32, name=f"raised{first_block}", tag=tags["raised"])
-            nc.scalar.activation(raised[:], scores, ACT.Relu, bias=floor_up[:])
-            base, over01, diff12, over2 = (
-                keep.tile([P, count], F32, name=f"{name}{first_block}", tag=tags.get(name, f"{name}{first_block}"), align_bytes=64)
-                for name in ("base", "over01", "diff12", "over2")
+        expd = keep.tile([P, BLOCKS, D], F32, name="expd")
+        for b in (2, 3, 1, 0):
+            nc.scalar.activation(
+                expd[:, b, :], scores[:, :, b], ACT.Exp, bias=low[:, b : b + 1], accum_out=den[:, b : b + 1]
             )
-            if first_block:
-                low = keep.tile([P, count], F32, name="low_direct", tag="w_grouped1", align_bytes=64)
-            else:
-                low = keep.tile([P, count], F32, name="low0", tag="low0", align_bytes=64)
-            expd = keep.tile([P, count, D], F32, name=f"expd{first_block}", tag=tags["expd"])
-            cols = [slice(b, b + 1) for b in range(count)]
-            for c in cols:
-                nc.scalar.activation(over01[:, c], raised[:, 1, c], ACT.Relu, bias=raised[:, 0, c], scale=-1.0)
-                nc.scalar.activation(diff12[:, c], raised[:, 2, c], ACT.Identity, bias=raised[:, 1, c], scale=-1.0)
-            nc.scalar.activation(base[:], raised[:, 2, :], ACT.Identity, bias=floor_up[:], scale=-1.0)
-            for c in cols:
-                nc.scalar.activation(over2[:, c], over01[:, c], ACT.Relu, bias=diff12[:, c])
-            for c in cols:
-                nc.scalar.activation(low[:, c], over2[:, c], ACT.Identity, bias=base[:, c], scale=-1.0)
-            for b in range(count):
-                nc.scalar.activation(
-                    expd[:, b, :],
-                    scores[:, :, b],
-                    ACT.Exp,
-                    bias=low[:, b : b + 1],
-                    accum_out=den[:, first_block + b : first_block + b + 1],
-                )
-            return expd
 
-        half = V // 2
-        turned_blocks = half // P
+        def spread(bank, columns):
+            for i, column in enumerate(columns):
+                nc.tensor.transpose(bank[:, i * P : (i + 1) * P], column.to_broadcast([P, P]), ident[:])
 
-        def spread(bank, column):
-            for b in range(turned_blocks, BLOCKS):
-                c0 = (b - turned_blocks) * P
-                nc.tensor.transpose(bank[:, c0 : c0 + P], column(b).to_broadcast([P, P]), ident[:])
-
-        expd_direct = exponentials(turned_blocks, BLOCKS - turned_blocks, {"raised": "raised_direct", "expd": "expd_direct"})
         w_codes, w_planes = [], []
         for z in range(PASSES):
             grouped = keep.tile([P, N, PACK], BF16, name=f"w_grouped{z}", tag=f"w_grouped{z}", align_bytes=64)
@@ -158,14 +132,12 @@ def tile_picked_gatv_relu_p_kernel(
             )
 
         exp_rows = []
-        for first_d, count, tag in ((0, 2, "bank5"), (2, 1, "bank6")):
-            bank = psum.tile([P, count, half], F32, name=f"exp_bank{first_d}", tag=tag)
-            for i in range(count):
-                spread(bank[:, i, :], lambda b: expd_direct[:, b - turned_blocks, first_d + i : first_d + i + 1])
-            rows = keep.tile([P, count, half], F32, name=f"exp_rows{first_d}")
+        for tag, terms in (("bank5", [(0, 2), (0, 3), (1, 2), (1, 3)]), ("bank6", [(2, 1), (2, 2), (2, 3)])):
+            bank = psum.tile([P, len(terms) * P], F32, name=f"exp_{tag}", tag=tag)
+            spread(bank, [expd[:, b, d : d + 1] for d, b in terms])
+            rows = keep.tile([P, len(terms) * P], F32, name=f"exp_rows_{tag}")
             nc.scalar.copy(rows[:], bank[:])
-            exp_rows.extend(rows[:, i, :] for i in range(count))
-        expd_turned = exponentials(0, turned_blocks, {"raised": "expd_direct", "expd": "expd_turned"})
+            exp_rows.append(rows)
 
         def x_plane(z, g0, gw):
             h = 0 if g0 < parts[1][0] else 1
@@ -173,20 +145,19 @@ def tile_picked_gatv_relu_p_kernel(
             return x_planes[h][:, z * w + g0 - c0 : z * w + g0 - c0 + gw]
 
         groups = [(0, 512), (512, 128), (640, 128), (768, 128), (896, 128)]
-        spare = psum.tile([P, 512], F32, name="spare", tag="bank3")
-        banks = [psum.tile([P, w], F32, name=f"y_bank{g}", tag=f"bank{g}") for g, (c0, w) in enumerate(groups)]
-        y = keep.tile([P, S], F32, name="y", tag="low0", align_bytes=64)
+        spare = psum.tile([P, 256], F32, name="spare", tag="bank3")
+        banks = [psum.tile([P, w], F32, name=f"y_bank{g}", tag=f"bank{g or 6}") for g, (c0, w) in enumerate(groups)]
+        y = keep.tile([P, S], F32, name="y")
         steps = [(0, 0, 512), (0, 512, 512), (1, 0, 512), (1, 512, 256), (1, 768, 256)]
         picked_tiles = {
             (1, c0): reused.tile([P, 2 * w], U8, name=f"picked1_{c0}", offset=2 * c0, align_bytes=64)[:]
             for z, c0, w in steps
             if z == 1
         }
-        picked_tiles[0, 0] = keep.tile([P, S], U8, name="picked0_0", align_bytes=64)[:]
-        picked_tiles[0, 512] = keep.tile([P, S], U8, name="picked0_512", tag="w_raw0", align_bytes=64)[:]
-        inv = keep.tile([P, BLOCKS], F32, name="inv")
-        att = keep.tile([P, turned_blocks, D], F32, name="att")
-        nc.vector.reciprocal(inv[:], den[:])
+        picked_tiles[0, 0] = early.tile([P, S], U8, name="picked0_0", offset=320, align_bytes=64)[:]
+        picked_tiles[0, 512] = early.tile([P, S], U8, name="picked0_512", offset=1344, align_bytes=64)[:]
+        inv = reused.tile([P, BLOCKS], F32, name="inv", offset=2 * 512, align_bytes=64)
+        att = keep.tile([P, D], F32, name="att")
         seen = set()
         for z, c0, w in steps:
             picked = picked_tiles[z, c0]
@@ -214,72 +185,65 @@ def tile_picked_gatv_relu_p_kernel(
                             out=spare[:],
                             lhsT=w_codes[0][:].bitcast(FP8X4),
                             lhsT_scale=w_planes[0][:],
-                            rhs=first_words.bitcast(FP4X4),
-                            rhs_scale=x_plane(0, 0, 512),
+                            rhs=first_words[:, 0:512].bitcast(FP4X4),
+                            rhs_scale=x_plane(0, 0, 256),
                             start=True,
                             stop=True,
                         )
+                    if closing and g == 2:
+                        nc.vector.reciprocal(inv[:], den[:])
                     if closing and g == 3:
-                        nc.vector.tensor_tensor(
-                            att[:],
-                            expd_turned[:],
-                            inv[:, 0:turned_blocks].unsqueeze(2).to_broadcast([P, turned_blocks, D]),
-                            ALU.mult,
-                        )
+                        nc.vector.tensor_scalar(att[:], expd[:, 0, :], inv[:, 0:1], None, ALU.mult)
                     if closing and g in (1, 2, 3):
                         nc.vector.tensor_copy(y[:, g0 : g0 + gw], banks[g][:])
                     elif closing:
                         nc.scalar.copy(y[:, g0 : g0 + gw], banks[g][:])
 
-        inv_rows = psum.tile([P, half], F32, name="inv_rows", tag="bank4")
-        spread(inv_rows[:], lambda b: inv[:, b : b + 1])
+        inv_rows = psum.tile([P, (BLOCKS - 1) * P], F32, name="inv_rows", tag="bank3")
+        spread(inv_rows, [inv[:, b : b + 1] for b in range(1, BLOCKS)])
 
-        sums = [psum.tile([P, P], F32, name=f"sum{b}", tag=f"bank{2 + b}") for b in range(turned_blocks)]
+        def neighbours(d, c0, w):
+            return y[:].indirect(pos_sb[d][:, c0 // LIST_ROWS : (c0 + w) // LIST_ROWS])
+
+        turned_terms = [(1, 0), (1, 1), (0, 0), (0, 1), (0, 2)]
         turned = []
-        for d in range(D):
-            fetched = keep.tile([P, half], F32, name=f"fetched{d}")
-            on_scalar = half if d < D - 1 else P
-            nc.scalar.activation(fetched[:, 0:on_scalar], y[:].indirect(pos_sb[d][:, 0 : on_scalar // LIST_ROWS]), ACT.Copy)
-            if on_scalar < half:
-                nc.vector.tensor_copy(
-                    fetched[:, on_scalar:half], y[:].indirect(pos_sb[d][:, on_scalar // LIST_ROWS : half // LIST_ROWS])
-                )
-            if d < D - 1:
-                bank = psum.tile([P, turned_blocks, P], F32, name=f"turned{d}", tag=f"bank{d}")
-                turned.append([bank[:, b, :] for b in range(turned_blocks)])
-            else:
-                turned.append([psum.tile([P, P], F32, name=f"turned{d}_{b}", tag=f"bank{5 + b}")[:] for b in range(turned_blocks)])
-            for b in range(turned_blocks):
-                nc.tensor.transpose(turned[d][b], fetched[:, b * P : (b + 1) * P], ident[:])
-        for d in range(D):
-            for b in reversed(range(turned_blocks)):
-                weighted = keep.tile([P, P], F32, name=f"weighted{d}_{b}", tag=f"weighted{d}_{b}")
-                nc.scalar.activation(weighted[:], turned[d][b], ACT.Copy, scale=att[:, b, d : d + 1])
-                nc.tensor.matmul(sums[b][:], weighted[:], ident[:], start=(d == 0), stop=(d == D - 1), is_transpose=True)
+        for (b, d), bank in zip(turned_terms, (5, 7, 0, 1, 2)):
+            fetched = keep.tile([P, P], F32, name=f"fetched{b}_{d}")
+            nc.scalar.activation(fetched[:], neighbours(d, b * P, P), ACT.Copy)
+            turned.append(psum.tile([P, P], F32, name=f"turned{b}_{d}", tag=f"bank{bank}"))
+            nc.tensor.transpose(turned[-1][:], fetched[:], ident[:])
+        sums = [psum.tile([P, P], F32, name=f"sum{b}", tag=f"bank{4 + 2 * b}") for b in range(2)]
+        for (b, d), term in zip(turned_terms, turned):
+            weighted = keep.tile([P, P], F32, name=f"weighted{b}_{d}", tag=f"weighted{b}_{d}")
+            scale = att[:, d : d + 1] if b == 0 else expd[:, 1, d : d + 1]
+            nc.scalar.activation(weighted[:], term[:], ACT.Copy, scale=scale)
+            nc.tensor.matmul(sums[b][:], weighted[:], ident[:], start=(d == 0), stop=(d == D - 1 - b), is_transpose=True)
 
-        def fetch(d):
-            term = keep.tile([P, half], F32, name=f"term{d}")
-            nc.vector.tensor_tensor(
-                term[:], y[:].indirect(pos_sb[d][:, half // LIST_ROWS : V // LIST_ROWS]), exp_rows[d], ALU.mult
-            )
+        def fetch(d, c0, w, weights):
+            term = keep.tile([P, w], F32, name=f"term{d}_{c0}")
+            nc.vector.tensor_tensor(term[:], neighbours(d, c0, w), weights, ALU.mult)
             return term
 
-        terms = [fetch(d) for d in range(D)]
-        pieces = [(0, 128), (128, 64), (192, 64)]
-        sums_so_far = [terms[0][:, c0 : c0 + w] for c0, w in pieces]
-        for d in range(1, D):
-            total = keep.tile([P, half], F32, name=f"total{d}")
-            for i, (c0, w) in enumerate(pieces):
-                nc.vector.tensor_tensor(total[:, c0 : c0 + w], sums_so_far[i], terms[d][:, c0 : c0 + w], ALU.add)
-                sums_so_far[i] = total[:, c0 : c0 + w]
-        result = keep.tile([P, half], F32, name="result")
-        for i, (c0, w) in enumerate(pieces):
-            nc.vector.scalar_tensor_tensor(
-                result[:, c0 : c0 + w], sums_so_far[i], 0.0, inv_rows[:, c0 : c0 + w], ALU.max, ALU.mult
-            )
-        nc.sync.dma_start(out[:, half:V], result[:])
+        def clip(tile, total, b):
+            nc.vector.scalar_tensor_tensor(tile, total, 0.0, inv_rows[:, (b - 1) * P : b * P], ALU.max, ALU.mult)
 
-        clipped = keep.tile([P, half], F32, name="clipped")
-        for b in reversed(range(turned_blocks)):
-            nc.scalar.activation(clipped[:, b * P : (b + 1) * P], sums[b][:], ACT.Relu)
-        nc.sync.dma_start(out[:, 0:half], clipped[:])
+        half = V // 2
+        terms = [fetch(0, half, half, exp_rows[0][:, 0:half]), fetch(1, half, half, exp_rows[0][:, half:V])]
+        terms.append(fetch(2, half, half, exp_rows[1][:, P : P + half]))
+        pair = keep.tile([P, half], F32, name="pair")
+        nc.vector.tensor_tensor(pair[:], terms[0][:], terms[1][:], ALU.add)
+        last_term = fetch(2, P, P, exp_rows[1][:, 0:P])
+        total = keep.tile([P, half], F32, name="total")
+        for c0 in (0, P):
+            nc.vector.tensor_tensor(total[:, c0 : c0 + P], pair[:, c0 : c0 + P], terms[2][:, c0 : c0 + P], ALU.add)
+        results = [keep.tile([P, P], F32, name=f"result{b}", tag="weighted1_1" if b == 3 else f"result{b}") for b in range(BLOCKS)]
+        clip(results[2][:], total[:, 0:P], 2)
+        nc.sync.dma_start(out[:, 2 * P : 3 * P], results[2][:])
+        mixed = keep.tile([P, P], F32, name="mixed")
+        nc.vector.tensor_tensor(mixed[:], sums[1][:], last_term[:], ALU.add)
+        clip(results[3][:], total[:, P : 2 * P], 3)
+        nc.sync.dma_start(out[:, 3 * P : 4 * P], results[3][:])
+        clip(results[1][:], mixed[:], 1)
+        nc.sync.dma_start(out[:, P : 2 * P], results[1][:])
+        nc.scalar.activation(results[0][:], sums[0][:], ACT.Relu)
+        nc.sync.dma_start(out[:, 0:P], results[0][:])

@@ -144,9 +144,9 @@ def tile_picked_gatv_relu_p_kernel(
             c0, w = parts[h]
             return x_planes[h][:, z * w + g0 - c0 : z * w + g0 - c0 + gw]
 
-        groups = [(0, 512), (512, 128), (640, 128), (768, 128), (896, 128)]
+        groups = [(0, 256), (256, 256), (512, 128), (640, 128), (768, 128), (896, 128)]
         spare = psum.tile([P, 256], F32, name="spare", tag="bank3")
-        banks = [psum.tile([P, w], F32, name=f"y_bank{g}", tag=f"bank{g or 6}") for g, (c0, w) in enumerate(groups)]
+        banks = [psum.tile([P, w], F32, name=f"y_bank{g}", tag=f"bank{(5, 6, 1, 2, 3, 4)[g]}") for g, (c0, w) in enumerate(groups)]
         y = keep.tile([P, S], F32, name="y")
         steps = [(0, 0, 512), (0, 512, 512), (1, 0, 512), (1, 512, 256), (1, 768, 256)]
         picked_tiles = {
@@ -180,7 +180,7 @@ def tile_picked_gatv_relu_p_kernel(
                     )
                     if (z, g) == (0, 0):
                         first_words = picked
-                    if (z, g) == (0, 2):
+                    if (z, g) == (0, 3):
                         nc.tensor.matmul_mx(
                             out=spare[:],
                             lhsT=w_codes[0][:].bitcast(FP8X4),
@@ -190,11 +190,11 @@ def tile_picked_gatv_relu_p_kernel(
                             start=True,
                             stop=True,
                         )
-                    if closing and g == 2:
-                        nc.vector.reciprocal(inv[:], den[:])
                     if closing and g == 3:
+                        nc.vector.reciprocal(inv[:], den[:])
+                    if closing and g == 4:
                         nc.vector.tensor_scalar(att[:], expd[:, 0, :], inv[:, 0:1], None, ALU.mult)
-                    if closing and g in (1, 2, 3):
+                    if closing and g in (2, 3, 4):
                         nc.vector.tensor_copy(y[:, g0 : g0 + gw], banks[g][:])
                     elif closing:
                         nc.scalar.copy(y[:, g0 : g0 + gw], banks[g][:])
@@ -236,14 +236,13 @@ def tile_picked_gatv_relu_p_kernel(
         total = keep.tile([P, half], F32, name="total")
         for c0 in (0, P):
             nc.vector.tensor_tensor(total[:, c0 : c0 + P], pair[:, c0 : c0 + P], terms[2][:, c0 : c0 + P], ALU.add)
-        results = [keep.tile([P, P], F32, name=f"result{b}", tag="weighted1_1" if b == 3 else f"result{b}") for b in range(BLOCKS)]
-        clip(results[2][:], total[:, 0:P], 2)
-        nc.sync.dma_start(out[:, 2 * P : 3 * P], results[2][:])
+        upper = keep.tile([P, half], F32, name="upper")
+        clip(upper[:, 0:P], total[:, 0:P], 2)
         mixed = keep.tile([P, P], F32, name="mixed")
         nc.vector.tensor_tensor(mixed[:], sums[1][:], last_term[:], ALU.add)
-        clip(results[3][:], total[:, P : 2 * P], 3)
-        nc.sync.dma_start(out[:, 3 * P : 4 * P], results[3][:])
-        clip(results[1][:], mixed[:], 1)
-        nc.sync.dma_start(out[:, P : 2 * P], results[1][:])
-        nc.scalar.activation(results[0][:], sums[0][:], ACT.Relu)
-        nc.sync.dma_start(out[:, 0:P], results[0][:])
+        clip(upper[:, P:half], total[:, P:half], 3)
+        nc.sync.dma_start(out[:, half:V], upper[:])
+        lower = keep.tile([P, half], F32, name="lower")
+        clip(lower[:, P:half], mixed[:], 1)
+        nc.scalar.activation(lower[:, 0:P], sums[0][:], ACT.Relu)
+        nc.sync.dma_start(out[:, 0:half], lower[:])

@@ -109,7 +109,7 @@ def tile_picked_gatv_relu_p_kernel(
 
         den = keep.tile([P, BLOCKS], F32, name="den")
         expd = keep.tile([P, BLOCKS, D], F32, name="expd")
-        for b in (2, 3, 1, 0):
+        for b in (2, 3, 0, 1):
             nc.scalar.activation(
                 expd[:, b, :], scores[:, :, b], ACT.Exp, bias=low[:, b : b + 1], accum_out=den[:, b : b + 1]
             )
@@ -132,7 +132,7 @@ def tile_picked_gatv_relu_p_kernel(
             )
 
         exp_rows = []
-        for tag, terms in (("bank5", [(0, 2), (0, 3), (1, 2), (1, 3)]), ("bank6", [(2, 1), (2, 2), (2, 3)])):
+        for tag, terms in (("bank5", [(0, 2), (0, 3), (1, 2), (1, 3)]), ("bank6", [(2, 2), (2, 3)])):
             bank = psum.tile([P, len(terms) * P], F32, name=f"exp_{tag}", tag=tag)
             spread(bank, [expd[:, b, d : d + 1] for d, b in terms])
             rows = keep.tile([P, len(terms) * P], F32, name=f"exp_rows_{tag}")
@@ -157,7 +157,7 @@ def tile_picked_gatv_relu_p_kernel(
         picked_tiles[0, 0] = early.tile([P, S], U8, name="picked0_0", offset=320, align_bytes=64)[:]
         picked_tiles[0, 512] = early.tile([P, S], U8, name="picked0_512", offset=1344, align_bytes=64)[:]
         inv = reused.tile([P, BLOCKS], F32, name="inv", offset=2 * 512, align_bytes=64)
-        att = keep.tile([P, D], F32, name="att")
+        att = keep.tile([P, 2, D], F32, name="att")
         seen = set()
         for z, c0, w in steps:
             picked = picked_tiles[z, c0]
@@ -193,56 +193,64 @@ def tile_picked_gatv_relu_p_kernel(
                     if closing and g == 3:
                         nc.vector.reciprocal(inv[:], den[:])
                     if closing and g == 4:
-                        nc.vector.tensor_scalar(att[:], expd[:, 0, :], inv[:, 0:1], None, ALU.mult)
+                        nc.vector.tensor_tensor(
+                            att[:], expd[:, 0:2, :], inv[:, 0:2].unsqueeze(2).to_broadcast([P, 2, D]), ALU.mult
+                        )
                     if closing and g in (2, 3, 4):
                         nc.vector.tensor_copy(y[:, g0 : g0 + gw], banks[g][:])
                     elif closing:
                         nc.scalar.copy(y[:, g0 : g0 + gw], banks[g][:])
 
-        inv_rows = psum.tile([P, (BLOCKS - 1) * P], F32, name="inv_rows", tag="bank3")
-        spread(inv_rows, [inv[:, b : b + 1] for b in range(1, BLOCKS)])
+        half = V // 2
+        inv_rows = psum.tile([P, half], F32, name="inv_rows", tag="bank3")
+        spread(inv_rows, [inv[:, b : b + 1] for b in (2, 3)])
 
         def neighbours(d, c0, w):
             return y[:].indirect(pos_sb[d][:, c0 // LIST_ROWS : (c0 + w) // LIST_ROWS])
 
-        turned_terms = [(1, 0), (1, 1), (0, 0), (0, 1), (0, 2)]
-        turned = []
-        for (b, d), bank in zip(turned_terms, (5, 7, 0, 1, 2)):
-            fetched = keep.tile([P, P], F32, name=f"fetched{b}_{d}")
-            nc.scalar.activation(fetched[:], neighbours(d, b * P, P), ACT.Copy)
-            turned.append(psum.tile([P, P], F32, name=f"turned{b}_{d}", tag=f"bank{bank}"))
-            nc.tensor.transpose(turned[-1][:], fetched[:], ident[:])
+        fetched = [keep.tile([P, half], F32, name=f"fetched{d}", tag=f"fetched{d}") for d in range(D)]
+        nc.vector.tensor_copy(fetched[2][:, P:half], neighbours(2, P, P))
+        for d in range(D):
+            w = half if d < D - 1 else P
+            nc.scalar.activation(fetched[d][:, 0:w], neighbours(d, 0, w), ACT.Copy)
+        turned = {}
+        for d, tag in ((0, "bank0"), (1, "bank1")):
+            bank = psum.tile([P, 2, P], F32, name=f"turned{d}", tag=tag)
+            turned.update({(b, d): bank[:, b, :] for b in range(2)})
+        for b, tag in ((0, "bank5"), (1, "bank7")):
+            turned[b, 2] = psum.tile([P, P], F32, name=f"turned2_{b}", tag=tag)[:]
+        for d in range(D):
+            for b in range(2):
+                nc.tensor.transpose(turned[b, d], fetched[d][:, b * P : (b + 1) * P], ident[:])
         sums = [psum.tile([P, P], F32, name=f"sum{b}", tag=f"bank{4 + 2 * b}") for b in range(2)]
-        for (b, d), term in zip(turned_terms, turned):
-            weighted = keep.tile([P, P], F32, name=f"weighted{b}_{d}", tag=f"weighted{b}_{d}")
-            scale = att[:, d : d + 1] if b == 0 else expd[:, 1, d : d + 1]
-            nc.scalar.activation(weighted[:], term[:], ACT.Copy, scale=scale)
-            nc.tensor.matmul(sums[b][:], weighted[:], ident[:], start=(d == 0), stop=(d == D - 1 - b), is_transpose=True)
+        for d in range(D):
+            for b in (1, 0):
+                weighted = keep.tile([P, P], F32, name=f"weighted{b}_{d}")
+                nc.scalar.activation(weighted[:], turned[b, d], ACT.Copy, scale=att[:, b, d : d + 1])
+                nc.tensor.matmul(sums[b][:], weighted[:], ident[:], start=(d == 0), stop=(d == D - 1), is_transpose=True)
 
         def fetch(d, c0, w, weights):
-            term = keep.tile([P, w], F32, name=f"term{d}_{c0}")
-            nc.vector.tensor_tensor(term[:], neighbours(d, c0, w), weights, ALU.mult)
+            term = keep.tile([P, w], F32, name=f"term{d}_{c0}", tag="fetched1" if c0 else f"term{d}")
+            nc.vector.tensor_tensor(term[:], neighbours(d, half + c0, w), weights, ALU.mult)
             return term
 
-        def clip(tile, total, b):
-            nc.vector.scalar_tensor_tensor(tile, total, 0.0, inv_rows[:, (b - 1) * P : b * P], ALU.max, ALU.mult)
-
-        half = V // 2
-        terms = [fetch(0, half, half, exp_rows[0][:, 0:half]), fetch(1, half, half, exp_rows[0][:, half:V])]
-        terms.append(fetch(2, half, half, exp_rows[1][:, P : P + half]))
+        first_terms = [fetch(d, 0, half, exp_rows[0][:, d * half : (d + 1) * half]) for d in range(2)]
+        last_terms = [fetch(2, 0, P, exp_rows[1][:, 0:P])]
         pair = keep.tile([P, half], F32, name="pair")
-        nc.vector.tensor_tensor(pair[:], terms[0][:], terms[1][:], ALU.add)
-        last_term = fetch(2, P, P, exp_rows[1][:, 0:P])
+        nc.vector.tensor_tensor(pair[:], first_terms[0][:], first_terms[1][:], ALU.add)
+        last_terms.append(fetch(2, P, P, exp_rows[1][:, P:half]))
         total = keep.tile([P, half], F32, name="total")
-        for c0 in (0, P):
-            nc.vector.tensor_tensor(total[:, c0 : c0 + P], pair[:, c0 : c0 + P], terms[2][:, c0 : c0 + P], ALU.add)
         upper = keep.tile([P, half], F32, name="upper")
-        clip(upper[:, 0:P], total[:, 0:P], 2)
-        mixed = keep.tile([P, P], F32, name="mixed")
-        nc.vector.tensor_tensor(mixed[:], sums[1][:], last_term[:], ALU.add)
-        clip(upper[:, P:half], total[:, P:half], 3)
+        cols = [slice(0, P), slice(P, half)]
+        pieces = [(0, 128), (128, 64), (192, 64)]
+        for c0, w in pieces:
+            term = last_terms[c0 // P][:, c0 % P : c0 % P + w]
+            nc.vector.tensor_tensor(total[:, c0 : c0 + w], pair[:, c0 : c0 + w], term, ALU.add)
+        for c in (slice(c0, c0 + w) for c0, w in pieces):
+            nc.vector.scalar_tensor_tensor(upper[:, c], total[:, c], 0.0, inv_rows[:, c], ALU.max, ALU.mult)
         nc.sync.dma_start(out[:, half:V], upper[:])
+
         lower = keep.tile([P, half], F32, name="lower")
-        clip(lower[:, P:half], mixed[:], 1)
-        nc.scalar.activation(lower[:, 0:P], sums[0][:], ACT.Relu)
+        for b in (1, 0):
+            nc.scalar.activation(lower[:, cols[b]], sums[b][:], ACT.Relu)
         nc.sync.dma_start(out[:, 0:half], lower[:])

@@ -24,6 +24,7 @@ PASSES = K // (P * PACK)
 LIST_ROWS = 16
 SCALE_ROWS = 16
 BLOCKS = V // P
+MARGIN = 32.0
 
 
 def tile_picked_gatv_relu_p_kernel(
@@ -85,15 +86,27 @@ def tile_picked_gatv_relu_p_kernel(
         for planes in x_planes:
             nc.vector.memset(planes[:].bitcast(I32), 0)
 
-        score_bank = psum.tile([P, D, P], F32, name="score_bank", tag="bank7")
+        margin = keep.tile([P, 1], F32, name="margin")
+        nc.vector.memset(margin[:], -MARGIN)
+        lowered_bank = psum.tile([P, D, P], F32, name="lowered_bank", tag="bank7")
+        for d in range(D - 1):
+            nc.tensor.matmul(
+                lowered_bank[:, d, :], margin[:].to_broadcast([P, P]), ident[:], start=(d == 0), stop=False, is_transpose=True
+            )
+        for d in range(D):
+            nc.tensor.matmul(
+                lowered_bank[:, d, :], score_rows[:, d, :], ident[:], start=False, stop=(d == D - 1), is_transpose=True
+            )
+        score_bank = psum.tile([P, D, P], F32, name="score_bank", tag="bank0")
         for d in range(D):
             nc.tensor.transpose(score_bank[:, d, :], score_rows[:, d, :], ident[:])
         scores = score_bank[:, :, live:P]
+        lowered = lowered_bank[:, :, live:P]
         low = keep.tile([P, BLOCKS], F32, name="low", tag="w_grouped1", align_bytes=64)
 
         for h, (c0, w) in enumerate(parts):
             if h == 1:
-                nc.vector.tensor_reduce(low[:], scores.rearrange("p d b -> p b d"), AXIS.X, ALU.max, negate=True)
+                nc.vector.tensor_reduce(low[:], lowered.rearrange("p d b -> p b d"), AXIS.X, ALU.max, negate=True)
                 picked_scales = early.tile([P, w], U8, name="picked_scales1", offset=64, align_bytes=64)
             else:
                 picked_scales = keep.tile([P, w], U8, name="picked_scales0", align_bytes=64)
@@ -132,7 +145,7 @@ def tile_picked_gatv_relu_p_kernel(
             )
 
         exp_rows = []
-        for tag, terms in (("bank5", [(0, 2), (0, 3), (1, 2), (1, 3)]), ("bank6", [(2, 2), (2, 3)])):
+        for tag, terms in (("bank5", [(0, 2), (0, 3)]), ("bank6", [(1, 2), (1, 3)])):
             bank = psum.tile([P, len(terms) * P], F32, name=f"exp_{tag}", tag=tag)
             spread(bank, [expd[:, b, d : d + 1] for d, b in terms])
             rows = keep.tile([P, len(terms) * P], F32, name=f"exp_rows_{tag}")
@@ -208,49 +221,45 @@ def tile_picked_gatv_relu_p_kernel(
         def neighbours(d, c0, w):
             return y[:].indirect(pos_sb[d][:, c0 // LIST_ROWS : (c0 + w) // LIST_ROWS])
 
+        own = 128
         fetched = [keep.tile([P, half], F32, name=f"fetched{d}", tag=f"fetched{d}") for d in range(D)]
-        nc.vector.tensor_copy(fetched[2][:, P:half], neighbours(2, P, P))
+        nc.vector.tensor_copy(fetched[2][:, own:half], neighbours(2, own, half - own))
         for d in range(D):
-            w = half if d < D - 1 else P
+            w = half if d < D - 1 else own
             nc.scalar.activation(fetched[d][:, 0:w], neighbours(d, 0, w), ACT.Copy)
-        turned = {}
-        for d, tag in ((0, "bank0"), (1, "bank1")):
-            bank = psum.tile([P, 2, P], F32, name=f"turned{d}", tag=tag)
-            turned.update({(b, d): bank[:, b, :] for b in range(2)})
-        for b, tag in ((0, "bank5"), (1, "bank7")):
-            turned[b, 2] = psum.tile([P, P], F32, name=f"turned2_{b}", tag=tag)[:]
-        for d in range(D):
-            for b in range(2):
-                nc.tensor.transpose(turned[b, d], fetched[d][:, b * P : (b + 1) * P], ident[:])
+        first_bank = psum.tile([P, 2, P], F32, name="turned0", tag="bank0")
+        turned = {(b, 0): first_bank[:, b, :] for b in range(2)}
+        for (b, d), tag in (((1, 2), "bank7"), ((1, 1), "bank2"), ((0, 1), "bank1"), ((0, 2), "bank5")):
+            turned[b, d] = psum.tile([P, P], F32, name=f"turned{d}_{b}", tag=tag)[:]
+        for b, d in turned:
+            nc.tensor.transpose(turned[b, d], fetched[d][:, b * P : (b + 1) * P], ident[:])
         sums = [psum.tile([P, P], F32, name=f"sum{b}", tag=f"bank{4 + 2 * b}") for b in range(2)]
-        for d in range(D):
-            for b in (1, 0):
-                weighted = keep.tile([P, P], F32, name=f"weighted{b}_{d}")
-                nc.scalar.activation(weighted[:], turned[b, d], ACT.Copy, scale=att[:, b, d : d + 1])
-                nc.tensor.matmul(sums[b][:], weighted[:], ident[:], start=(d == 0), stop=(d == D - 1), is_transpose=True)
+        summed = [0, 0]
+        for b, d in turned:
+            weighted = keep.tile([P, P], F32, name=f"weighted{b}_{d}")
+            nc.scalar.activation(weighted[:], turned[b, d], ACT.Copy, scale=att[:, b, d : d + 1])
+            nc.tensor.matmul(
+                sums[b][:], weighted[:], ident[:], start=(summed[b] == 0), stop=(summed[b] == D - 1), is_transpose=True
+            )
+            summed[b] += 1
 
-        def fetch(d, c0, w, weights):
-            term = keep.tile([P, w], F32, name=f"term{d}_{c0}", tag="fetched1" if c0 else f"term{d}")
-            nc.vector.tensor_tensor(term[:], neighbours(d, half + c0, w), weights, ALU.mult)
+        def fused(name, d, c0, w, other, op):
+            term = keep.tile([P, w], F32, name=name)
+            nc.vector.tensor_tensor(term[:], neighbours(d, half + c0, w), other, op)
             return term
 
-        first_terms = [fetch(d, 0, half, exp_rows[0][:, d * half : (d + 1) * half]) for d in range(2)]
-        last_terms = [fetch(2, 0, P, exp_rows[1][:, 0:P])]
-        pair = keep.tile([P, half], F32, name="pair")
-        nc.vector.tensor_tensor(pair[:], first_terms[0][:], first_terms[1][:], ALU.add)
-        last_terms.append(fetch(2, P, P, exp_rows[1][:, P:half]))
-        total = keep.tile([P, half], F32, name="total")
-        upper = keep.tile([P, half], F32, name="upper")
         cols = [slice(0, P), slice(P, half)]
-        pieces = [(0, 128), (128, 64), (192, 64)]
-        for c0, w in pieces:
-            term = last_terms[c0 // P][:, c0 % P : c0 % P + w]
-            nc.vector.tensor_tensor(total[:, c0 : c0 + w], pair[:, c0 : c0 + w], term, ALU.add)
-        for c in (slice(c0, c0 + w) for c0, w in pieces):
-            nc.vector.scalar_tensor_tensor(upper[:, c], total[:, c], 0.0, inv_rows[:, c], ALU.max, ALU.mult)
-        nc.sync.dma_start(out[:, half:V], upper[:])
-
-        lower = keep.tile([P, half], F32, name="lower")
+        first = fused("first", 0, 0, half, exp_rows[0][:], ALU.mult)
+        second = [fused(f"second{i}", 1, c.start, P, exp_rows[1][:, c], ALU.mult) for i, c in enumerate(cols)]
+        pairs = []
+        for i, c in enumerate(cols):
+            pairs.append(keep.tile([P, P], F32, name=f"pair{i}"))
+            nc.vector.tensor_tensor(pairs[i][:], first[:, c], second[i][:], ALU.add)
+        wholes = [fused(f"whole{i}", 2, c.start, P, pairs[i][:], ALU.add) for i, c in enumerate(cols)]
+        results = [keep.tile([P, P], F32, name=f"result{b}") for b in range(BLOCKS)]
+        for i, c in enumerate(cols):
+            nc.vector.scalar_tensor_tensor(results[2 + i][:], wholes[i][:], 0.0, inv_rows[:, c], ALU.max, ALU.mult)
         for b in (1, 0):
-            nc.scalar.activation(lower[:, cols[b]], sums[b][:], ACT.Relu)
-        nc.sync.dma_start(out[:, 0:half], lower[:])
+            nc.scalar.activation(results[b][:], sums[b][:], ACT.Relu)
+        for b, queue in ((1, nc.sync), (2, nc.sync), (3, nc.sync), (0, nc.scalar)):
+            queue.dma_start(out[:, b * P : (b + 1) * P], results[b][:])

@@ -221,7 +221,7 @@ def tile_picked_gatv_relu_p_kernel(
         def neighbours(d, c0, w):
             return y[:].indirect(pos_sb[d][:, c0 // LIST_ROWS : (c0 + w) // LIST_ROWS])
 
-        own = 128
+        own = 64
         fetched = [keep.tile([P, half], F32, name=f"fetched{d}", tag=f"fetched{d}") for d in range(D)]
         nc.vector.tensor_copy(fetched[2][:, own:half], neighbours(2, own, half - own))
         for d in range(D):

@@ -224,16 +224,16 @@ def tile_picked_gatv_relu_p_kernel(
         own = 64
         fetched = [keep.tile([P, half], F32, name=f"fetched{d}", tag=f"fetched{d}") for d in range(D)]
         nc.vector.tensor_copy(fetched[2][:, own:half], neighbours(2, own, half - own))
-        for d in range(D):
-            w = half if d < D - 1 else own
-            nc.scalar.activation(fetched[d][:, 0:w], neighbours(d, 0, w), ACT.Copy)
-        first_bank = psum.tile([P, 2, P], F32, name="turned0", tag="bank0")
-        turned = {(b, 0): first_bank[:, b, :] for b in range(2)}
-        for (b, d), tag in (((1, 2), "bank7"), ((1, 1), "bank2"), ((0, 1), "bank1"), ((0, 2), "bank5")):
+        for d, c0, w in ((0, 0, half), (1, P, P), (1, 0, P), (2, 0, own)):
+            nc.scalar.activation(fetched[d][:, c0 : c0 + w], neighbours(d, c0, w), ACT.Copy)
+        turned = {}
+        for (b, d), tag in (
+            ((1, 2), "bank7"), ((1, 0), "bank0"), ((1, 1), "bank2"), ((0, 0), "bank4"), ((0, 1), "bank1"), ((0, 2), "bank5")
+        ):
             turned[b, d] = psum.tile([P, P], F32, name=f"turned{d}_{b}", tag=tag)[:]
         for b, d in turned:
             nc.tensor.transpose(turned[b, d], fetched[d][:, b * P : (b + 1) * P], ident[:])
-        sums = [psum.tile([P, P], F32, name=f"sum{b}", tag=f"bank{4 + 2 * b}") for b in range(2)]
+        sums = [psum.tile([P, P], F32, name=f"sum{b}", tag=("bank7", "bank6")[b]) for b in range(2)]
         summed = [0, 0]
         for b, d in turned:
             weighted = keep.tile([P, P], F32, name=f"weighted{b}_{d}")

@@ -106,8 +106,7 @@ def tile_picked_gatv_relu_p_kernel(
 
         for h, (c0, w) in enumerate(parts):
             if h == 1:
-                nc.vector.tensor_reduce(low[:], lowered.rearrange("p d b -> p b d"), AXIS.X, ALU.max, negate=True)
-                picked_scales = early.tile([P, w], U8, name="picked_scales1", offset=64, align_bytes=64)
+                picked_scales = keep.tile([P, w], U8, name="picked_scales1", align_bytes=64)
             else:
                 picked_scales = keep.tile([P, w], U8, name="picked_scales0", align_bytes=64)
             nc.vector.tensor_copy(
@@ -120,6 +119,7 @@ def tile_picked_gatv_relu_p_kernel(
                     picked_scales[row : row + 8, :].bitcast(I32),
                 )
 
+        nc.vector.tensor_reduce(low[:], lowered.rearrange("p d b -> p b d"), AXIS.X, ALU.max, negate=True)
         den = keep.tile([P, BLOCKS], F32, name="den")
         expd = keep.tile([P, BLOCKS, D], F32, name="expd")
         for b in (2, 3, 0, 1):

from contextlib import ExitStack

import concourse.mybir as mybir
from concourse.masks import make_identity

K, T, S, D, V, N = 1024, 2048, 1024, 3, 512, 128
FLOPS = 2 * K * N * S

F32 = mybir.dt.float32
BF16 = mybir.dt.bfloat16
I32 = mybir.dt.int32
U32 = mybir.dt.uint32
U16 = mybir.dt.uint16
U8 = mybir.dt.uint8
FP8X4 = mybir.dt.float8_e4m3fn_x4
FP4X4 = mybir.dt.float4_e2m1fn_x4
ALU = mybir.AluOpType
ACT = mybir.ActivationFunctionType
AXIS = mybir.AxisListType

P = 128
PACK = 4
PASSES = K // (P * PACK)
LIST_ROWS = 16
SCALE_ROWS = 16
BLOCKS = V // P
MARGIN = 32.0


def tile_picked_gatv_relu_p_kernel(
    tc, x_words, x_scales, w1, score, offs, pos1, pos2, pos3, out
):
    nc = tc.nc
    with ExitStack() as ctx:
        keep = ctx.enter_context(tc.tile_pool(name="keep", bufs=1))
        psum = ctx.enter_context(tc.psum_pool(name="psum", bufs=1))
        reused = ctx.enter_context(tc.tile_pool(name="reused", bufs=1))
        early = ctx.enter_context(tc.tile_pool(name="early", bufs=1))

        ident = keep.tile([P, P], F32, name="ident")
        nc.vector.memset(ident[:], 0.0)
        make_identity(nc, ident[:], nomemset=True)
        offs_sb = keep.tile([P, S // LIST_ROWS], U16, name="offs_sb")

        first = P - PASSES * SCALE_ROWS
        scale_table = keep.tile([P, T], U8, name="scale_table", align_bytes=64)
        nc.sync.dma_start(
            scale_table[first:P, :].bitcast(I32),
            x_scales.rearrange("z q c -> q z c").bitcast(I32),
        )
        nc.sync.dma_start(offs_sb[:], offs)
        nc.vector.memset(scale_table[0:first, :].bitcast(I32), 0)

        live = P - BLOCKS
        score_rows = early.tile([P, D, P], F32, name="score_rows", offset=256, align_bytes=64)
        nc.sync.dma_start(score_rows[live:P], score[:, 0, :].rearrange("d (b n) -> b d n", n=P))
        nc.vector.memset(score_rows[0:live], 0.0)

        def load_list(d, pos):
            tile = keep.tile([P, V // LIST_ROWS], U16, name=f"pos_sb{d}")
            nc.sync.dma_start(tile[:], pos)
            return tile

        def load_words(z):
            table = keep.tile([P, 2 * T], U8, name=f"word_table{z}", tag=f"word_table{z}", align_bytes=64)
            nc.sync.dma_start(table[:].bitcast(I32), x_words[z].bitcast(I32))
            return table

        def load_weights(z):
            if z == 0:
                rows = early.tile([P, PACK, N], F32, name="w_raw0", offset=1792, align_bytes=64)
            else:
                rows = reused.tile([P, PACK, N], F32, name="w_raw1", offset=0, align_bytes=64)
            nc.sync.dma_start(rows[:], w1[z * P * PACK : (z + 1) * P * PACK, :].rearrange("(p j) m -> p j m", j=PACK))
            return rows

        w_raw, word_tables = [], []
        for z in range(PASSES):
            w_raw.append(load_weights(z))
            word_tables.append(load_words(z))

        pos_sb = [load_list(d, pos) for d, pos in enumerate((pos1, pos2, pos3))]

        parts = [(0, 768), (768, 256)]
        x_planes = [keep.tile([P, PASSES * w], U8, name=f"x_planes{c0}", align_bytes=64) for c0, w in parts]
        for planes in x_planes:
            nc.vector.memset(planes[:].bitcast(I32), 0)

        margin = keep.tile([P, 1], F32, name="margin")
        nc.vector.memset(margin[:], -MARGIN)
        lowered_bank = psum.tile([P, D, P], F32, name="lowered_bank", tag="bank7")
        for d in range(D - 1):
            nc.tensor.matmul(
                lowered_bank[:, d, :], margin[:].to_broadcast([P, P]), ident[:], start=(d == 0), stop=False, is_transpose=True
            )
        for d in range(D):
            nc.tensor.matmul(
                lowered_bank[:, d, :], score_rows[:, d, :], ident[:], start=False, stop=(d == D - 1), is_transpose=True
            )
        score_bank = psum.tile([P, D, P], F32, name="score_bank", tag="bank0")
        for d in range(D):
            nc.tensor.transpose(score_bank[:, d, :], score_rows[:, d, :], ident[:])
        scores = score_bank[:, :, live:P]
        lowered = lowered_bank[:, :, live:P]
        low = keep.tile([P, BLOCKS], F32, name="low", tag="w_grouped1", align_bytes=64)

        for h, (c0, w) in enumerate(parts):
            if h == 1:
                picked_scales = keep.tile([P, w], U8, name="picked_scales1", align_bytes=64)
            else:
                picked_scales = keep.tile([P, w], U8, name="picked_scales0", align_bytes=64)
            nc.vector.tensor_copy(
                picked_scales[:], scale_table[:].indirect(offs_sb[:, c0 // LIST_ROWS : (c0 + w) // LIST_ROWS])
            )
            for q in range(4):
                row = first + 8 * q
                nc.sync.dma_start(
                    x_planes[h][32 * q : 32 * q + 4, :].bitcast(I32),
                    picked_scales[row : row + 8, :].bitcast(I32),
                )

        nc.vector.tensor_reduce(low[:], lowered.rearrange("p d b -> p b d"), AXIS.X, ALU.max, negate=True)
        den = keep.tile([P, BLOCKS], F32, name="den")
        expd = keep.tile([P, BLOCKS, D], F32, name="expd")
        for b in (2, 3, 0, 1):
            nc.scalar.activation(
                expd[:, b, :], scores[:, :, b], ACT.Exp, bias=low[:, b : b + 1], accum_out=den[:, b : b + 1]
            )

        def spread(bank, columns):
            for i, column in enumerate(columns):
                nc.tensor.transpose(bank[:, i * P : (i + 1) * P], column.to_broadcast([P, P]), ident[:])

        w_codes, w_planes = [], []
        for z in range(PASSES):
            grouped = keep.tile([P, N, PACK], BF16, name=f"w_grouped{z}", tag=f"w_grouped{z}", align_bytes=64)
            nc.scalar.copy(
                grouped[:].rearrange("p (c i) j -> p c j i", i=PACK),
                w_raw[z][:].rearrange("p j (c i) -> p c j i", i=PACK),
            )
            w_codes.append(keep.tile([P, N], U32, name=f"w_codes{z}", align_bytes=64))
            w_planes.append(keep.tile([P, N], U8, name=f"w_planes{z}", align_bytes=64))
            nc.vector.quantize_mx(
                out=w_codes[z][:].bitcast(FP8X4), scales=w_planes[z][:], in_=grouped[:].rearrange("p m j -> p (m j)")
            )

        exp_rows = []
        for tag, terms in (("bank5", [(0, 2), (0, 3)]), ("bank6", [(1, 2), (1, 3)])):
            bank = psum.tile([P, len(terms) * P], F32, name=f"exp_{tag}", tag=tag)
            spread(bank, [expd[:, b, d : d + 1] for d, b in terms])
            rows = keep.tile([P, len(terms) * P], F32, name=f"exp_rows_{tag}")
            nc.scalar.copy(rows[:], bank[:])
            exp_rows.append(rows)

        def x_plane(z, g0, gw):
            h = 0 if g0 < parts[1][0] else 1
            c0, w = parts[h]
            return x_planes[h][:, z * w + g0 - c0 : z * w + g0 - c0 + gw]

        groups = [(0, 256), (256, 256), (512, 128), (640, 128), (768, 128), (896, 128)]
        spare = psum.tile([P, 256], F32, name="spare", tag="bank3")
        banks = [psum.tile([P, w], F32, name=f"y_bank{g}", tag=f"bank{(5, 6, 1, 2, 3, 4)[g]}") for g, (c0, w) in enumerate(groups)]
        y = keep.tile([P, S], F32, name="y")
        steps = [(0, 0, 512), (0, 512, 512), (1, 0, 512), (1, 512, 256), (1, 768, 256)]
        picked_tiles = {
            (1, c0): reused.tile([P, 2 * w], U8, name=f"picked1_{c0}", offset=2 * c0, align_bytes=64)[:]
            for z, c0, w in steps
            if z == 1
        }
        picked_tiles[0, 0] = early.tile([P, S], U8, name="picked0_0", offset=320, align_bytes=64)[:]
        picked_tiles[0, 512] = early.tile([P, S], U8, name="picked0_512", offset=1344, align_bytes=64)[:]
        inv = reused.tile([P, BLOCKS], F32, name="inv", offset=2 * 512, align_bytes=64)
        att = keep.tile([P, 2, D], F32, name="att")
        seen = set()
        for z, c0, w in steps:
            picked = picked_tiles[z, c0]
            nc.vector.tensor_copy(
                picked.bitcast(U16),
                word_tables[z][:].bitcast(U16).indirect(offs_sb[:, c0 // LIST_ROWS : (c0 + w) // LIST_ROWS]),
            )
            for g, (g0, gw) in enumerate(groups):
                if c0 <= g0 < c0 + w:
                    closing = g in seen
                    seen.add(g)
                    nc.tensor.matmul_mx(
                        out=banks[g][:],
                        lhsT=w_codes[z][:].bitcast(FP8X4),
                        lhsT_scale=w_planes[z][:],
                        rhs=picked[:, 2 * (g0 - c0) : 2 * (g0 - c0 + gw)].bitcast(FP4X4),
                        rhs_scale=x_plane(z, g0, gw),
                        start=not closing,
                        stop=closing,
                    )
                    if (z, g) == (0, 0):
                        first_words = picked
                    if (z, g) == (0, 3):
                        nc.tensor.matmul_mx(
                            out=spare[:],
                            lhsT=w_codes[0][:].bitcast(FP8X4),
                            lhsT_scale=w_planes[0][:],
                            rhs=first_words[:, 0:512].bitcast(FP4X4),
                            rhs_scale=x_plane(0, 0, 256),
                            start=True,
                            stop=True,
                        )
                    if closing and g == 3:
                        nc.vector.reciprocal(inv[:], den[:])
                    if closing and g == 4:
                        nc.vector.tensor_tensor(
                            att[:], expd[:, 0:2, :], inv[:, 0:2].unsqueeze(2).to_broadcast([P, 2, D]), ALU.mult
                        )
                    if closing and g in (2, 3, 4):
                        nc.vector.tensor_copy(y[:, g0 : g0 + gw], banks[g][:])
                    elif closing:
                        nc.scalar.copy(y[:, g0 : g0 + gw], banks[g][:])

        half = V // 2
        inv_rows = psum.tile([P, half], F32, name="inv_rows", tag="bank3")
        spread(inv_rows, [inv[:, b : b + 1] for b in (2, 3)])

        def neighbours(d, c0, w):
            return y[:].indirect(pos_sb[d][:, c0 // LIST_ROWS : (c0 + w) // LIST_ROWS])

        own = 64
        fetched = [keep.tile([P, half], F32, name=f"fetched{d}", tag=f"fetched{d}") for d in range(D)]
        nc.vector.tensor_copy(fetched[2][:, own:half], neighbours(2, own, half - own))
        for d, c0, w in ((0, 0, half), (1, P, P), (1, 0, P), (2, 0, own)):
            nc.scalar.activation(fetched[d][:, c0 : c0 + w], neighbours(d, c0, w), ACT.Copy)
        turned = {}
        for (b, d), tag in (
            ((1, 2), "bank7"), ((1, 0), "bank0"), ((1, 1), "bank2"), ((0, 0), "bank4"), ((0, 1), "bank1"), ((0, 2), "bank5")
        ):
            turned[b, d] = psum.tile([P, P], F32, name=f"turned{d}_{b}", tag=tag)[:]
        for b, d in turned:
            nc.tensor.transpose(turned[b, d], fetched[d][:, b * P : (b + 1) * P], ident[:])
        sums = [psum.tile([P, P], F32, name=f"sum{b}", tag=("bank7", "bank6")[b]) for b in range(2)]
        summed = [0, 0]
        for b, d in turned:
            weighted = keep.tile([P, P], F32, name=f"weighted{b}_{d}")
            nc.scalar.activation(weighted[:], turned[b, d], ACT.Copy, scale=att[:, b, d : d + 1])
            nc.tensor.matmul(
                sums[b][:], weighted[:], ident[:], start=(summed[b] == 0), stop=(summed[b] == D - 1), is_transpose=True
            )
            summed[b] += 1

        def fused(name, d, c0, w, other, op):
            term = keep.tile([P, w], F32, name=name)
            nc.vector.tensor_tensor(term[:], neighbours(d, half + c0, w), other, op)
            return term

        cols = [slice(0, P), slice(P, half)]
        first = fused("first", 0, 0, half, exp_rows[0][:], ALU.mult)
        second = [fused(f"second{i}", 1, c.start, P, exp_rows[1][:, c], ALU.mult) for i, c in enumerate(cols)]
        pairs = []
        for i, c in enumerate(cols):
            pairs.append(keep.tile([P, P], F32, name=f"pair{i}"))
            nc.vector.tensor_tensor(pairs[i][:], first[:, c], second[i][:], ALU.add)
        wholes = [fused(f"whole{i}", 2, c.start, P, pairs[i][:], ALU.add) for i, c in enumerate(cols)]
        results = [keep.tile([P, P], F32, name=f"result{b}") for b in range(BLOCKS)]
        for i, c in enumerate(cols):
            nc.vector.scalar_tensor_tensor(results[2 + i][:], wholes[i][:], 0.0, inv_rows[:, c], ALU.max, ALU.mult)
        for b in (1, 0):
            nc.scalar.activation(results[b][:], sums[b][:], ACT.Relu)
        for b, queue in ((1, nc.sync), (2, nc.sync), (3, nc.sync), (0, nc.scalar)):
            queue.dma_start(out[:, b * P : (b + 1) * P], results[b][:])
